import numpy as np
import ml_dtypes


def mxq(x, axis, fmt="e4m3"):
    dtype, down = {"e4m3": (ml_dtypes.float8_e4m3fn, 7), "e5m2": (ml_dtypes.float8_e5m2, 14)}[fmt]
    v = np.moveaxis(np.asarray(x, np.float32).astype(ml_dtypes.bfloat16).astype(np.float64), axis, -1)
    blocks = v.reshape(v.shape[:-1] + (-1, 32))
    amax = np.abs(blocks).max(-1, keepdims=True)
    byte = np.maximum(np.where(amax > 0, np.frexp(amax)[1] - 1 + 127, 0) - down, 1)
    scale = np.exp2(byte - 127.0)
    codes = (blocks / scale).astype(np.float32).astype(dtype).astype(np.float64)
    return np.moveaxis((codes * scale).reshape(v.shape), -1, axis)


WIDE = False


def mx_kscale(k):
    if not WIDE:
        return np.ones(k)
    levels = np.array([10, -10, 5, -5, 0])
    if k % 512:
        return np.exp2(np.random.permutation(np.resize(levels, k // 32))).repeat(32)
    a = np.empty((k // 512, 16))
    for p in range(k // 512):
        a[p, :8] = np.random.permutation(np.resize(levels, 8))
        for g in range(8):
            far = levels[np.abs(levels - a[p, g]) >= 10]
            a[p, g + 8] = far[np.random.randint(len(far))]
    return np.exp2(a.ravel()).repeat(32)


def f64(x):
    return np.asarray(x).astype(np.float64)


def striped(idx):
    return np.tile(idx.reshape(-1, 16).T, (8, 1)).astype(np.uint16)


def unstriped(offs):
    return offs[:16].T.reshape(-1).astype(np.int64)


E2M1 = np.array([0.0, 0.5, 1.0, 1.5, 2.0, 3.0, 4.0, 6.0, -0.0, -0.5, -1.0, -1.5, -2.0, -3.0, -4.0, -6.0])


def pack_weight(w, fmt):
    k, n = w.shape
    w = f64(np.asarray(w, np.float32).astype(ml_dtypes.bfloat16)).reshape(k // 32, 32, n)
    amax = np.abs(w).max(1)
    if fmt == "e4m3":
        byte = np.frexp(amax)[1] - 1 + 127 - 7
    else:
        mant, ex = np.frexp(amax / 6.0)
        byte = np.where(mant > 0.5, ex, ex - 1) + 127
    byte = np.clip(np.where(amax > 0, byte, 1), 1, 254)
    scaled = (w * np.exp2(127.0 - byte)[:, None, :]).reshape(k, n).astype(np.float32)
    by_word = np.ascontiguousarray(scaled.reshape(k // 512, 128, 4, n).transpose(0, 1, 3, 2))
    if fmt == "e4m3":
        words = by_word.astype(ml_dtypes.float8_e4m3fn).view(np.uint8)
    else:
        c = by_word.astype(ml_dtypes.float4_e2m1fn).view(np.uint8) & 0xF
        words = (c[..., 0::2] | (c[..., 1::2] << 4)).reshape(k // 512, 128, 2 * n)
    return np.ascontiguousarray(words), np.ascontiguousarray(byte.astype(np.uint8).reshape(k // 512, 16, n))


def unpack_weight(words, scales, fmt):
    g, _, n = scales.shape
    words = np.ascontiguousarray(words).reshape(g, 128, n, -1)
    if fmt == "e4m3":
        vals = words.view(ml_dtypes.float8_e4m3fn).astype(np.float64)
    else:
        nib = np.empty((g, 128, n, 4), np.uint8)
        nib[..., 0::2] = words & 0xF
        nib[..., 1::2] = words >> 4
        vals = E2M1[nib]
    vals = vals * np.repeat(np.exp2(scales.astype(np.float64) - 127.0), 8, axis=1)[..., None]
    return vals.transpose(0, 1, 3, 2).reshape(g * 512, n)


def gelu(v):
    return 0.5 * v * (1.0 + np.tanh(np.sqrt(2.0 / np.pi) * (v + 0.044715 * v**3)))


K, T, E1, C1, E2, C2, H = 1024, 1024, 8, 128, 8, 128, 512
N = 512


def deal(E, C):
    slot_token = np.random.permutation(T)
    return slot_token, None, np.random.uniform(0.2, 1.0, T)


def by_expert(wq, xq, E, C):
    return np.concatenate([wq[e].T @ xq[:, e * C:(e + 1) * C] for e in range(E)], axis=1)


def setup_inputs():
    n = np.random.standard_normal
    s = mx_kscale(K)
    u = mx_kscale(H)
    slots1, pos1, g1 = deal(E1, C1)
    slots2, pos2, g2 = deal(E2, C2)
    x = pack_weight(n((K, T)) * s[:, None], "e4m3")
    w1 = [pack_weight(m, "e2m1") for m in n((E1, K, H)) / np.sqrt(K) / s[None, :, None] * u]
    w2 = [pack_weight(m, "e2m1") for m in n((E2, H, N)) / np.sqrt(H) / u[None, :, None]]
    return {
        "x_words": x[0],
        "x_scales": x[1],
        "w1_words": np.stack([m[0] for m in w1]),
        "w1_scales": np.stack([m[1] for m in w1]),
        "w2_words": np.stack([m[0] for m in w2]),
        "w2_scales": np.stack([m[1] for m in w2]),
        "gate1": (np.tile(g1, (128, 1))).astype(np.float32),
        "gate2": (np.tile(g2, (128, 1))).astype(np.float32),
        "offs": striped(slots1),
        "offs2": striped(slots2),
    }


def reference(x_words, x_scales, w1_words, w1_scales, w2_words, w2_scales, gate1, gate2, offs, offs2):
    w1 = np.stack([unpack_weight(w1_words[e], w1_scales[e], "e2m1") for e in range(E1)])
    w2 = np.stack([unpack_weight(w2_words[e], w2_scales[e], "e2m1") for e in range(E2)])
    idx, idx2 = unstriped(offs), unstriped(offs2)
    xq = unpack_weight(x_words, x_scales, "e4m3")[:, idx]
    h = gelu(by_expert(w1, xq, E1, C1))
    c = np.zeros((H, T))
    c[:, idx] = f64(gate1[:1]) * h
    y = by_expert(w2, mxq(c[:, idx2], 0, "e4m3"), E2, C2)
    out = np.zeros((N, T))
    out[:, idx2] = f64(gate2[:1]) * y
    return out

@@ -1,0 +1,218 @@
+from contextlib import ExitStack
+
+import concourse.mybir as mybir
+from concourse.masks import make_identity
+
+P = 128
+T = 1024
+E = 8
+C = 128
+K, H, N = 1024, 512, 512
+FLOPS = 2 * T * (K * H + H * N)
+
+F32 = mybir.dt.float32
+BF16 = mybir.dt.bfloat16
+I32 = mybir.dt.int32
+U32 = mybir.dt.uint32
+U16 = mybir.dt.uint16
+U8 = mybir.dt.uint8
+FP8X4 = mybir.dt.float8_e4m3fn_x4
+FP4X4 = mybir.dt.float4_e2m1fn_x4
+ACT = mybir.ActivationFunctionType
+MULT = mybir.AluOpType.mult
+
+
+def runs(*sizes):
+    edges = [sum(sizes[:i]) for i in range(len(sizes) + 1)]
+    return [range(a, b) for a, b in zip(edges, edges[1:])]
+
+
+XS_RUNS = runs(4,4)
+XW_RUNS = runs(1,1,2,4)
+W1_RUNS = runs(1,1,2,4)
+S1_RUNS = runs(2,6)
+C_RUNS = runs(1,3,4)
+G_RUNS = runs(1,1,2,4)
+Y_RUNS = runs(1,1,2,4)
+
+
+def tile_moe_ser_gelu_kernel(
+    tc, x_words, x_scales, w1_words, w1_scales, w2_words, w2_scales, gate1, gate2, offs, offs2, out
+):
+    nc = tc.nc
+
+    def entries(lst, run):
+        return lst[:, run.start * C // 16 : run.stop * C // 16]
+
+    def slots(run):
+        return slice(run.start * C, run.stop * C)
+
+    def place(e, run):
+        return slice((e - run.start) * C, (e - run.start + 1) * C)
+
+    with ExitStack() as ctx:
+        lists = ctx.enter_context(tc.tile_pool(name="lists", bufs=1))
+        keep = ctx.enter_context(tc.tile_pool(name="keep", bufs=1))
+        ring = ctx.enter_context(tc.tile_pool(name="ring", bufs=3))
+        psum = ctx.enter_context(tc.psum_pool(name="psum", bufs=2))
+
+        list1 = lists.tile([P, T // 16], U16, name="list1")
+        list2 = lists.tile([P, T // 16], U16, name="list2")
+        nc.sync.dma_start(list1[:], offs)
+
+        xs = keep.tile([P, T], U8, name="xs", align_bytes=64)
+        nc.vector.memset(xs[:].bitcast(I32), 0)
+        w1s_tiles = [keep.tile([P, 2 * len(run), H], U8, name=f"w1s{run.start}", align_bytes=64) for run in S1_RUNS]
+        w2s = keep.tile([P, E, N], U8, name="w2s", align_bytes=64)
+        nc.vector.memset(w1s_tiles[0][:].rearrange("p a n -> p (a n)").bitcast(I32), 0)
+        ident = keep.tile([P, P], F32, name="ident")
+        make_identity(nc, ident[:])
+        nc.gpsimd.memset(w1s_tiles[1][:].rearrange("p a n -> p (a n)").bitcast(I32), 0)
+        nc.gpsimd.memset(w2s[:].rearrange("p a n -> p (a n)").bitcast(I32), 0)
+        warm = keep.tile([P, 8], F32, name="warm")
+        nc.scalar.activation(warm[:], ident[:, 0:8], ACT.Gelu_apprx_tanh)
+
+        for q in range(2):
+            nc.sync.dma_start(xs[32 * q : 32 * q + 8, :].bitcast(I32), x_scales[:, 4 * q : 4 * q + 4, :].bitcast(I32))
+        for q in range(2, 4):
+            for s in range(2):
+                first = 32 * q - 4 * s
+                nc.sync.dma_start(xs[first : first + 4, :].bitcast(I32), x_scales[s, 4 * q : 4 * q + 4, :].bitcast(I32))
+        xw = [keep.tile([P, T], I32, name=f"xw{s}") for s in range(2)]
+        for s in range(2):
+            nc.sync.dma_start(xw[s][:], x_words[s].rearrange("p t d -> p (t d)").bitcast(I32))
+
+        def load_planes(tile, scales):
+            rows = scales.rearrange("e s (q r) n -> r q (e s) n", r=4)
+            for r in range(4):
+                nc.sync.dma_start(tile[r:P:32, :, :].bitcast(I32), rows[r].bitcast(I32))
+
+        g1_rows = keep.tile([P, C], F32, name="g1_rows")
+        w1w = {}
+        w1s = {e: tile[:, 2 * (e - run.start) : 2 * (e - run.start) + 2, :] for run, tile in zip(S1_RUNS, w1s_tiles) for e in run}
+        load_planes(w1s_tiles[0], w1_scales[S1_RUNS[0].start : S1_RUNS[0].stop])
+        for run in W1_RUNS:
+            tile = keep.tile([P, 2 * len(run), 2 * H], U8, name=f"w1w{run.start}", align_bytes=64)
+            nc.sync.dma_start(
+                tile[:].bitcast(I32), w1_words[run.start : run.stop].rearrange("e s p n -> p (e s) n").bitcast(I32)
+            )
+            for e in run:
+                w1w[e] = tile[:, 2 * (e - run.start) : 2 * (e - run.start) + 2, :]
+            if run.stop == 1:
+                nc.sync.dma_start(g1_rows[:], gate1[0:16, :].rearrange("r (e u) -> (r e) u", u=C))
+            if run.stop == S1_RUNS[1].start:
+                load_planes(w1s_tiles[1], w1_scales[S1_RUNS[1].start : S1_RUNS[1].stop])
+        nc.sync.dma_start(list2[:], offs2)
+        load_planes(w2s, w2_scales)
+        w2w = keep.tile([P, E, 2 * N], U8, name="w2w", align_bytes=64)
+        nc.sync.dma_start(w2w[:].bitcast(I32), w2_words.rearrange("e s p n -> p (e s) n").bitcast(I32))
+        g2 = keep.tile([P, T], F32, name="g2")
+        nc.sync.dma_start(g2[:], gate2)
+
+        xs_slot = {}
+        for run in XS_RUNS:
+            gathered = keep.tile([P, len(run) * C], U8, name=f"xs_pass0_{run.start}", align_bytes=64)
+            shifted = keep.tile([P, len(run) * C], U8, name=f"xs_pass1_{run.start}", align_bytes=64)
+            nc.vector.tensor_copy(gathered[:], xs[:].indirect(entries(list1, run)))
+            nc.scalar.dma_start(shifted[0:64, :].bitcast(I32), gathered[4:68, :].bitcast(I32))
+            nc.scalar.dma_start(shifted[64:128, :].bitcast(I32), gathered[60:124, :].bitcast(I32))
+            for e in run:
+                xs_slot[e, 0] = gathered[:, place(e, run)]
+                xs_slot[e, 1] = shifted[:, place(e, run)]
+        xw_slot = {}
+        for run in XW_RUNS:
+            for s in range(2):
+                tile = keep.tile([P, len(run) * C], U32, name=f"xw_slot{run.start}_{s}", align_bytes=64)
+                nc.vector.tensor_copy(tile[:], xw[s][:].bitcast(U32).indirect(entries(list1, run)))
+                for e in run:
+                    xw_slot[e, s] = tile[:, place(e, run)]
+
+        turned = psum.tile([P, 4, C], F32, name="turned")
+        nc.tensor.transpose(turned[:, 0, :], g1_rows[:], ident[:])
+        g1 = keep.tile([P, E], F32, name="g1")
+        nc.scalar.copy(g1[:], turned[:, 0, 0:E])
+
+        h_slot = []
+        for run in C_RUNS:
+            tile = keep.tile([P, 4, len(run) * C], F32, name=f"h_slot{run.start}")
+            h_slot.append(tile)
+            for e in run:
+                sums = psum.tile([P, H], F32, name="sums1", bufs=3)
+                for s in range(2):
+                    nc.tensor.matmul_mx(
+                        out=sums[:],
+                        lhsT=xw_slot[e, s].bitcast(FP8X4),
+                        lhsT_scale=xs_slot[e, s],
+                        rhs=w1w[e][:, s, :].bitcast(FP4X4),
+                        rhs_scale=w1s[e][:, s, :],
+                        start=(s == 0),
+                        stop=(s == 1),
+                    )
+                h = ring.tile([P, 4, P], F32, name="h")
+                nc.scalar.activation(h[:], sums[:].rearrange("m (p t) -> m t p", t=4), ACT.Gelu_apprx_tanh)
+                gated = ring.tile([P, 4, P], F32, name="gated")
+                nc.scalar.activation(gated[:], h[:], ACT.Copy, scale=g1[:, e : e + 1])
+                h = gated
+                turned = psum.tile([P, 4, C], F32, name="turned")
+                for t in range(4):
+                    nc.tensor.transpose(turned[:, t, :], h[:, t, :], ident[:])
+                nc.scalar.copy(tile[:, :, place(e, run)], turned[:])
+
+        c_tok = [keep.tile([P, T], F32, name=f"c_tok{t}") for t in range(4)]
+        for a, t in [[0, 0], [0, 1], [0, 2], [0, 3], [1, 0], [1, 1], [2, 0], [2, 1], [1, 2], [2, 2], [1, 3], [2, 3]]:
+            nc.vector.tensor_copy(c_tok[t][:].indirect(entries(list1, C_RUNS[a])), h_slot[a][:, t, :])
+
+        y_tiles = [keep.tile([P, 4, len(run) * C], F32, name=f"y{run.start}") for run in Y_RUNS]
+        y = {f: tile[:, :, place(f, run)] for run, tile in zip(Y_RUNS, y_tiles) for f in run}
+        grouped = [keep.tile([P, len(run) * C, 4], BF16, name=f"grouped{run.start}", align_bytes=64) for run in G_RUNS]
+        c_bf = [keep.tile([P, T], BF16, name=f"c_bf{t}") for t in range(4)]
+
+        def gather_scalar(a, t):
+            nc.scalar.activation(grouped[a][:, :, t], c_bf[t][:].indirect(entries(list2, G_RUNS[a])), ACT.Copy)
+
+        def gather_vector(a, t):
+            nc.vector.tensor_copy(grouped[a][:, :, t], c_tok[t][:].indirect(entries(list2, G_RUNS[a])))
+
+        def experts2(a):
+            run = G_RUNS[a]
+            codes = keep.tile([P, len(run) * C], U32, name=f"codes{run.start}", align_bytes=64)
+            scales = keep.tile([P, len(run) * C], U8, name=f"scales{run.start}", align_bytes=64)
+            nc.vector.quantize_mx(
+                out=codes[:].bitcast(FP8X4), scales=scales[:], in_=grouped[a][:].rearrange("p m t -> p (m t)")
+            )
+            for f in run:
+                for blocks in runs(1, 3) if f == 0 else runs(4):
+                    sums = psum.tile([P, len(blocks), C], F32, name="sums2", bufs=3)
+                    for b in blocks:
+                        nc.tensor.matmul_mx(
+                            out=sums[:, b - blocks.start, :],
+                            lhsT=w2w[:, f, 2 * P * b : 2 * P * (b + 1)].bitcast(FP4X4),
+                            lhsT_scale=w2s[:, f, P * b : P * (b + 1)],
+                            rhs=codes[:, place(f, run)].bitcast(FP8X4),
+                            rhs_scale=scales[:, place(f, run)],
+                            start=True,
+                            stop=True,
+                        )
+                    nc.scalar.copy(y[f][:, blocks.start : blocks.stop, :], sums[:])
+
+        for t in range(3):
+            nc.scalar.copy(c_bf[t][:], c_tok[t][:])
+            for a in range(len(G_RUNS)):
+                if t < 2 or a >= 1:
+                    gather_scalar(a, t)
+        for a in range(1):
+            for t in range(2, 4):
+                gather_vector(a, t)
+            if a == 0:
+                nc.scalar.copy(c_bf[3][:], c_tok[3][:])
+            experts2(a)
+        for a in range(1, len(G_RUNS)):
+            gather_scalar(a, 3)
+            experts2(a)
+
+        out_tok = [keep.tile([P, T], F32, name=f"out_tok{b}") for b in range(4)]
+        for run, tile in zip(Y_RUNS, y_tiles):
+            for b in range(4):
+                nc.vector.tensor_tensor(out_tok[b][:].indirect(entries(list2, run)), tile[:, b, :], g2[:, slots(run)], MULT)
+                if run.stop == E:
+                    nc.sync.dma_start(out[P * b : P * (b + 1), :], out_tok[b][:])

@@ -28,11 +28,11 @@ def runs(*sizes):
 
 
 XS_RUNS = runs(4,4)
-XW_RUNS = runs(1,1,2,4)
+XW_RUNS = runs(1,3,4)
 W1_RUNS = runs(1,1,2,4)
 S1_RUNS = runs(2,6)
-C_RUNS = runs(1,3,4)
-G_RUNS = runs(1,1,2,4)
+C_RUNS = runs(1,1,2,4)
+G_RUNS = runs(1,1,2,2,2)
 Y_RUNS = runs(1,1,2,4)
 
 
@@ -59,9 +59,12 @@ def tile_moe_ser_gelu_kernel(
         list1 = lists.tile([P, T // 16], U16, name="list1")
         list2 = lists.tile([P, T // 16], U16, name="list2")
         nc.sync.dma_start(list1[:], offs)
+        warm = keep.tile([P, 16], F32, name="warm")
+        nc.gpsimd.memset(warm[:, 0:8], 0.0)
+        nc.scalar.activation(warm[:, 8:16], warm[:, 0:8], ACT.Gelu_apprx_tanh)
 
         xs = keep.tile([P, T], U8, name="xs", align_bytes=64)
-        nc.vector.memset(xs[:].bitcast(I32), 0)
+        nc.gpsimd.memset(xs[:].bitcast(I32), 0)
         w1s_tiles = [keep.tile([P, 2 * len(run), H], U8, name=f"w1s{run.start}", align_bytes=64) for run in S1_RUNS]
         w2s = keep.tile([P, E, N], U8, name="w2s", align_bytes=64)
         nc.vector.memset(w1s_tiles[0][:].rearrange("p a n -> p (a n)").bitcast(I32), 0)
@@ -69,8 +72,6 @@ def tile_moe_ser_gelu_kernel(
         make_identity(nc, ident[:])
         nc.gpsimd.memset(w1s_tiles[1][:].rearrange("p a n -> p (a n)").bitcast(I32), 0)
         nc.gpsimd.memset(w2s[:].rearrange("p a n -> p (a n)").bitcast(I32), 0)
-        warm = keep.tile([P, 8], F32, name="warm")
-        nc.scalar.activation(warm[:], ident[:, 0:8], ACT.Gelu_apprx_tanh)
 
         for q in range(2):
             nc.sync.dma_start(xs[32 * q : 32 * q + 8, :].bitcast(I32), x_scales[:, 4 * q : 4 * q + 4, :].bitcast(I32))
@@ -87,7 +88,7 @@ def tile_moe_ser_gelu_kernel(
             for r in range(4):
                 nc.sync.dma_start(tile[r:P:32, :, :].bitcast(I32), rows[r].bitcast(I32))
 
-        g1_rows = keep.tile([P, C], F32, name="g1_rows")
+        g1 = keep.tile([P, T], F32, name="g1")
         w1w = {}
         w1s = {e: tile[:, 2 * (e - run.start) : 2 * (e - run.start) + 2, :] for run, tile in zip(S1_RUNS, w1s_tiles) for e in run}
         load_planes(w1s_tiles[0], w1_scales[S1_RUNS[0].start : S1_RUNS[0].stop])
@@ -99,7 +100,7 @@ def tile_moe_ser_gelu_kernel(
             for e in run:
                 w1w[e] = tile[:, 2 * (e - run.start) : 2 * (e - run.start) + 2, :]
             if run.stop == 1:
-                nc.sync.dma_start(g1_rows[:], gate1[0:16, :].rearrange("r (e u) -> (r e) u", u=C))
+                nc.sync.dma_start(g1[:], gate1)
             if run.stop == S1_RUNS[1].start:
                 load_planes(w1s_tiles[1], w1_scales[S1_RUNS[1].start : S1_RUNS[1].stop])
         nc.sync.dma_start(list2[:], offs2)
@@ -127,11 +128,6 @@ def tile_moe_ser_gelu_kernel(
                 for e in run:
                     xw_slot[e, s] = tile[:, place(e, run)]
 
-        turned = psum.tile([P, 4, C], F32, name="turned")
-        nc.tensor.transpose(turned[:, 0, :], g1_rows[:], ident[:])
-        g1 = keep.tile([P, E], F32, name="g1")
-        nc.scalar.copy(g1[:], turned[:, 0, 0:E])
-
         h_slot = []
         for run in C_RUNS:
             tile = keep.tile([P, 4, len(run) * C], F32, name=f"h_slot{run.start}")
@@ -150,22 +146,21 @@ def tile_moe_ser_gelu_kernel(
                     )
                 h = ring.tile([P, 4, P], F32, name="h")
                 nc.scalar.activation(h[:], sums[:].rearrange("m (p t) -> m t p", t=4), ACT.Gelu_apprx_tanh)
-                gated = ring.tile([P, 4, P], F32, name="gated")
-                nc.scalar.activation(gated[:], h[:], ACT.Copy, scale=g1[:, e : e + 1])
-                h = gated
                 turned = psum.tile([P, 4, C], F32, name="turned")
                 for t in range(4):
                     nc.tensor.transpose(turned[:, t, :], h[:, t, :], ident[:])
                 nc.scalar.copy(tile[:, :, place(e, run)], turned[:])
 
         c_tok = [keep.tile([P, T], F32, name=f"c_tok{t}") for t in range(4)]
-        for a, t in [[0, 0], [0, 1], [0, 2], [0, 3], [1, 0], [1, 1], [2, 0], [2, 1], [1, 2], [2, 2], [1, 3], [2, 3]]:
-            nc.vector.tensor_copy(c_tok[t][:].indirect(entries(list1, C_RUNS[a])), h_slot[a][:, t, :])
+        for a, t in [[0, 0], [0, 1], [0, 2], [0, 3], [1, 0], [1, 1], [1, 2], [1, 3], [2, 0], [2, 1], [2, 2], [3, 0], [3, 1], [2, 3], [3, 2], [3, 3]]:
+            nc.vector.tensor_tensor(
+                c_tok[t][:].indirect(entries(list1, C_RUNS[a])), h_slot[a][:, t, :], g1[:, slots(C_RUNS[a])], MULT
+            )
 
         y_tiles = [keep.tile([P, 4, len(run) * C], F32, name=f"y{run.start}") for run in Y_RUNS]
         y = {f: tile[:, :, place(f, run)] for run, tile in zip(Y_RUNS, y_tiles) for f in run}
         grouped = [keep.tile([P, len(run) * C, 4], BF16, name=f"grouped{run.start}", align_bytes=64) for run in G_RUNS]
-        c_bf = [keep.tile([P, T], BF16, name=f"c_bf{t}") for t in range(4)]
+        c_bf = [keep.tile([P, T], BF16, name=f"c_bf{t}") for t in range(3)]
 
         def gather_scalar(a, t):
             nc.scalar.activation(grouped[a][:, :, t], c_bf[t][:].indirect(entries(list2, G_RUNS[a])), ACT.Copy)
@@ -203,9 +198,10 @@ def tile_moe_ser_gelu_kernel(
         for a in range(1):
             for t in range(2, 4):
                 gather_vector(a, t)
-            if a == 0:
-                nc.scalar.copy(c_bf[3][:], c_tok[3][:])
             experts2(a)
+            if a == 0:
+                c_bf.append(keep.tile([P, T], BF16, name="grouped0", align_bytes=64))
+                nc.vector.tensor_copy(c_bf[3][:], c_tok[3][:])
         for a in range(1, len(G_RUNS)):
             gather_scalar(a, 3)
             experts2(a)

@@ -59,19 +59,17 @@ def tile_moe_ser_gelu_kernel(
         list1 = lists.tile([P, T // 16], U16, name="list1")
         list2 = lists.tile([P, T // 16], U16, name="list2")
         nc.sync.dma_start(list1[:], offs)
-        warm = keep.tile([P, 16], F32, name="warm")
-        nc.gpsimd.memset(warm[:, 0:8], 0.0)
-        nc.scalar.activation(warm[:, 8:16], warm[:, 0:8], ACT.Gelu_apprx_tanh)
 
         xs = keep.tile([P, T], U8, name="xs", align_bytes=64)
         nc.gpsimd.memset(xs[:].bitcast(I32), 0)
+        warm = keep.tile([P, 16], F32, name="warm")
+        nc.gpsimd.memset(warm[:, 0:8], 0.0)
+        nc.scalar.activation(warm[:, 8:16], warm[:, 0:8], ACT.Gelu_apprx_tanh)
         w1s_tiles = [keep.tile([P, 2 * len(run), H], U8, name=f"w1s{run.start}", align_bytes=64) for run in S1_RUNS]
-        w2s = keep.tile([P, E, N], U8, name="w2s", align_bytes=64)
         nc.vector.memset(w1s_tiles[0][:].rearrange("p a n -> p (a n)").bitcast(I32), 0)
         ident = keep.tile([P, P], F32, name="ident")
         make_identity(nc, ident[:])
-        nc.gpsimd.memset(w1s_tiles[1][:].rearrange("p a n -> p (a n)").bitcast(I32), 0)
-        nc.gpsimd.memset(w2s[:].rearrange("p a n -> p (a n)").bitcast(I32), 0)
+        nc.vector.memset(w1s_tiles[1][:].rearrange("p a n -> p (a n)").bitcast(I32), 0)
 
         for q in range(2):
             nc.sync.dma_start(xs[32 * q : 32 * q + 8, :].bitcast(I32), x_scales[:, 4 * q : 4 * q + 4, :].bitcast(I32))
@@ -79,9 +77,8 @@ def tile_moe_ser_gelu_kernel(
             for s in range(2):
                 first = 32 * q - 4 * s
                 nc.sync.dma_start(xs[first : first + 4, :].bitcast(I32), x_scales[s, 4 * q : 4 * q + 4, :].bitcast(I32))
-        xw = [keep.tile([P, T], I32, name=f"xw{s}") for s in range(2)]
-        for s in range(2):
-            nc.sync.dma_start(xw[s][:], x_words[s].rearrange("p t d -> p (t d)").bitcast(I32))
+        xw = keep.tile([P, 2, T], I32, name="xw")
+        nc.sync.dma_start(xw[:], x_words.rearrange("s p t d -> p s (t d)").bitcast(I32))
 
         def load_planes(tile, scales):
             rows = scales.rearrange("e s (q r) n -> r q (e s) n", r=4)
@@ -104,7 +101,6 @@ def tile_moe_ser_gelu_kernel(
             if run.stop == S1_RUNS[1].start:
                 load_planes(w1s_tiles[1], w1_scales[S1_RUNS[1].start : S1_RUNS[1].stop])
         nc.sync.dma_start(list2[:], offs2)
-        load_planes(w2s, w2_scales)
         w2w = keep.tile([P, E, 2 * N], U8, name="w2w", align_bytes=64)
         nc.sync.dma_start(w2w[:].bitcast(I32), w2_words.rearrange("e s p n -> p (e s) n").bitcast(I32))
         g2 = keep.tile([P, T], F32, name="g2")
@@ -124,7 +120,7 @@ def tile_moe_ser_gelu_kernel(
         for run in XW_RUNS:
             for s in range(2):
                 tile = keep.tile([P, len(run) * C], U32, name=f"xw_slot{run.start}_{s}", align_bytes=64)
-                nc.vector.tensor_copy(tile[:], xw[s][:].bitcast(U32).indirect(entries(list1, run)))
+                nc.vector.tensor_copy(tile[:], xw[:, s, :].bitcast(U32).indirect(entries(list1, run)))
                 for e in run:
                     xw_slot[e, s] = tile[:, place(e, run)]
 
@@ -144,15 +140,22 @@ def tile_moe_ser_gelu_kernel(
                         start=(s == 0),
                         stop=(s == 1),
                     )
-                h = ring.tile([P, 4, P], F32, name="h")
-                nc.scalar.activation(h[:], sums[:].rearrange("m (p t) -> m t p", t=4), ACT.Gelu_apprx_tanh)
-                turned = psum.tile([P, 4, C], F32, name="turned")
-                for t in range(4):
-                    nc.tensor.transpose(turned[:, t, :], h[:, t, :], ident[:])
-                nc.scalar.copy(tile[:, :, place(e, run)], turned[:])
+                for planes in runs(1, 3) if e == 0 else runs(4):
+                    part = slice(planes.start, planes.stop)
+                    h = ring.tile([P, len(planes), P], F32, name="h")
+                    nc.scalar.activation(
+                        h[:], sums[:].rearrange("m (p t) -> m t p", t=4)[:, part, :], ACT.Gelu_apprx_tanh
+                    )
+                    turned = psum.tile([P, len(planes), C], F32, name="turned")
+                    for t in range(len(planes)):
+                        nc.tensor.transpose(turned[:, t, :], h[:, t, :], ident[:])
+                    nc.scalar.copy(tile[:, part, place(e, run)], turned[:])
+
+        w2s = w1s_tiles[1][:, 0:E, :]
+        load_planes(w2s, w2_scales)
 
         c_tok = [keep.tile([P, T], F32, name=f"c_tok{t}") for t in range(4)]
-        for a, t in [[0, 0], [0, 1], [0, 2], [0, 3], [1, 0], [1, 1], [1, 2], [1, 3], [2, 0], [2, 1], [2, 2], [3, 0], [3, 1], [2, 3], [3, 2], [3, 3]]:
+        for a, t in [[0, 0], [0, 1], [0, 2], [0, 3], [1, 0], [1, 1], [1, 2], [1, 3], [2, 0], [2, 1], [3, 0], [2, 2], [3, 1], [2, 3], [3, 2], [3, 3]]:
             nc.vector.tensor_tensor(
                 c_tok[t][:].indirect(entries(list1, C_RUNS[a])), h_slot[a][:, t, :], g1[:, slots(C_RUNS[a])], MULT
             )

@@ -33,7 +33,7 @@ W1_RUNS = runs(1,1,2,4)
 S1_RUNS = runs(2,6)
 C_RUNS = runs(1,1,2,4)
 G_RUNS = runs(1,1,2,2,2)
-Y_RUNS = runs(1,1,2,4)
+Y_RUNS = runs(1,1,2,2,2)
 
 
 def tile_moe_ser_gelu_kernel(
@@ -163,10 +163,10 @@ def tile_moe_ser_gelu_kernel(
         y_tiles = [keep.tile([P, 4, len(run) * C], F32, name=f"y{run.start}") for run in Y_RUNS]
         y = {f: tile[:, :, place(f, run)] for run, tile in zip(Y_RUNS, y_tiles) for f in run}
         grouped = [keep.tile([P, len(run) * C, 4], BF16, name=f"grouped{run.start}", align_bytes=64) for run in G_RUNS]
-        c_bf = [keep.tile([P, T], BF16, name=f"c_bf{t}") for t in range(3)]
+        c_bf = [keep.tile([P, T], BF16, name=f"c_bf{t}")[:] for t in range(2)]
 
         def gather_scalar(a, t):
-            nc.scalar.activation(grouped[a][:, :, t], c_bf[t][:].indirect(entries(list2, G_RUNS[a])), ACT.Copy)
+            nc.scalar.activation(grouped[a][:, :, t], c_bf[t].indirect(entries(list2, G_RUNS[a])), ACT.Copy)
 
         def gather_vector(a, t):
             nc.vector.tensor_copy(grouped[a][:, :, t], c_tok[t][:].indirect(entries(list2, G_RUNS[a])))
@@ -193,21 +193,25 @@ def tile_moe_ser_gelu_kernel(
                         )
                     nc.scalar.copy(y[f][:, blocks.start : blocks.stop, :], sums[:])
 
-        for t in range(3):
-            nc.scalar.copy(c_bf[t][:], c_tok[t][:])
+        for t in range(2):
+            nc.scalar.copy(c_bf[t], c_tok[t][:])
             for a in range(len(G_RUNS)):
-                if t < 2 or a >= 1:
-                    gather_scalar(a, t)
-        for a in range(1):
-            for t in range(2, 4):
-                gather_vector(a, t)
-            experts2(a)
-            if a == 0:
-                c_bf.append(keep.tile([P, T], BF16, name="grouped0", align_bytes=64))
-                nc.vector.tensor_copy(c_bf[3][:], c_tok[3][:])
+                gather_scalar(a, t)
+        for t in range(2, 4):
+            gather_vector(0, t)
+        experts2(0)
+        late = keep.tile([P, 2, T], BF16, name="grouped0", align_bytes=64)
+        for t in range(2, 4):
+            c_bf.append(late[:, t - 2, :])
+            nc.vector.tensor_copy(c_bf[t], c_tok[t][:])
         for a in range(1, len(G_RUNS)):
-            gather_scalar(a, 3)
-            experts2(a)
+            for t in range(2, 4):
+                gather_scalar(a, t)
+            if a == 1:
+                experts2(a)
+            if a > 2:
+                experts2(a - 1)
+        experts2(len(G_RUNS) - 1)
 
         out_tok = [keep.tile([P, T], F32, name=f"out_tok{b}") for b in range(4)]
         for run, tile in zip(Y_RUNS, y_tiles):

@@ -31,7 +31,7 @@ XS_RUNS = runs(4,4)
 XW_RUNS = runs(1,3,4)
 W1_RUNS = runs(1,1,2,4)
 S1_RUNS = runs(2,6)
-C_RUNS = runs(1,1,2,4)
+C_RUNS = runs(1,1,2,2,2)
 G_RUNS = runs(1,1,2,2,2)
 Y_RUNS = runs(1,1,2,2,2)
 
@@ -67,6 +67,8 @@ def tile_moe_ser_gelu_kernel(
         nc.scalar.activation(warm[:, 8:16], warm[:, 0:8], ACT.Gelu_apprx_tanh)
         w1s_tiles = [keep.tile([P, 2 * len(run), H], U8, name=f"w1s{run.start}", align_bytes=64) for run in S1_RUNS]
         nc.vector.memset(w1s_tiles[0][:].rearrange("p a n -> p (a n)").bitcast(I32), 0)
+        g1_rows = keep.tile([P, P], F32, name="g1_rows")
+        nc.gpsimd.memset(g1_rows[:], 0.0)
         ident = keep.tile([P, P], F32, name="ident")
         make_identity(nc, ident[:])
         nc.vector.memset(w1s_tiles[1][:].rearrange("p a n -> p (a n)").bitcast(I32), 0)
@@ -85,7 +87,6 @@ def tile_moe_ser_gelu_kernel(
             for r in range(4):
                 nc.sync.dma_start(tile[r:P:32, :, :].bitcast(I32), rows[r].bitcast(I32))
 
-        g1 = keep.tile([P, T], F32, name="g1")
         w1w = {}
         w1s = {e: tile[:, 2 * (e - run.start) : 2 * (e - run.start) + 2, :] for run, tile in zip(S1_RUNS, w1s_tiles) for e in run}
         load_planes(w1s_tiles[0], w1_scales[S1_RUNS[0].start : S1_RUNS[0].stop])
@@ -97,7 +98,7 @@ def tile_moe_ser_gelu_kernel(
             for e in run:
                 w1w[e] = tile[:, 2 * (e - run.start) : 2 * (e - run.start) + 2, :]
             if run.stop == 1:
-                nc.sync.dma_start(g1[:], gate1)
+                nc.sync.dma_start(g1_rows[0:E, :], gate1[0:1, :].rearrange("o (e u) -> (o e) u", e=E))
             if run.stop == S1_RUNS[1].start:
                 load_planes(w1s_tiles[1], w1_scales[S1_RUNS[1].start : S1_RUNS[1].stop])
         nc.sync.dma_start(list2[:], offs2)
@@ -124,10 +125,15 @@ def tile_moe_ser_gelu_kernel(
                 for e in run:
                     xw_slot[e, s] = tile[:, place(e, run)]
 
-        h_slot = []
+        g1_turned = psum.tile([P, P], F32, name="turned")
+        nc.tensor.transpose(g1_turned[:], g1_rows[:], ident[:])
+        g1 = keep.tile([P, E], F32, name="g1")
+        nc.scalar.copy(g1[:], g1_turned[:, 0:E])
+
+        c_slot = []
         for run in C_RUNS:
-            tile = keep.tile([P, 4, len(run) * C], F32, name=f"h_slot{run.start}")
-            h_slot.append(tile)
+            tile = keep.tile([P, 2, len(run) * C], F32, name=f"c_slot{run.start}")
+            c_slot.append(tile)
             for e in run:
                 sums = psum.tile([P, H], F32, name="sums1", bufs=3)
                 for s in range(2):
@@ -140,43 +146,37 @@ def tile_moe_ser_gelu_kernel(
                         start=(s == 0),
                         stop=(s == 1),
                     )
-                for planes in runs(1, 3) if e == 0 else runs(4):
-                    part = slice(planes.start, planes.stop)
-                    h = ring.tile([P, len(planes), P], F32, name="h")
-                    nc.scalar.activation(
-                        h[:], sums[:].rearrange("m (p t) -> m t p", t=4)[:, part, :], ACT.Gelu_apprx_tanh
-                    )
-                    turned = psum.tile([P, len(planes), C], F32, name="turned")
-                    for t in range(len(planes)):
-                        nc.tensor.transpose(turned[:, t, :], h[:, t, :], ident[:])
-                    nc.scalar.copy(tile[:, part, place(e, run)], turned[:])
+                h = ring.tile([P, 2, P, 2], F32, name="h")
+                nc.scalar.activation(h[:], sums[:].rearrange("m (p u d) -> m u p d", u=2, d=2), ACT.Gelu_apprx_tanh)
+                c_rows = ring.tile([P, H], BF16, name="c_rows")
+                nc.scalar.activation(c_rows[:], h[:].rearrange("m u p d -> m (u p d)"), ACT.Copy, scale=g1[:, e : e + 1])
+                pairs = c_rows[:].bitcast(F32)
+                turned = psum.tile([P, 2, C], F32, name="turned")
+                for u in range(2):
+                    nc.tensor.transpose(turned[:, u, :], pairs[:, P * u : P * (u + 1)], ident[:])
+                nc.scalar.copy(tile[:, :, place(e, run)], turned[:])
 
         w2s = w1s_tiles[1][:, 0:E, :]
         load_planes(w2s, w2_scales)
 
-        c_tok = [keep.tile([P, T], F32, name=f"c_tok{t}") for t in range(4)]
-        for a, t in [[0, 0], [0, 1], [0, 2], [0, 3], [1, 0], [1, 1], [1, 2], [1, 3], [2, 0], [2, 1], [3, 0], [2, 2], [3, 1], [2, 3], [3, 2], [3, 3]]:
-            nc.vector.tensor_tensor(
-                c_tok[t][:].indirect(entries(list1, C_RUNS[a])), h_slot[a][:, t, :], g1[:, slots(C_RUNS[a])], MULT
-            )
+        c_tok = [keep.tile([P, T], F32, name=f"c_tok{u}") for u in range(2)]
+        for run, tile in zip(C_RUNS, c_slot):
+            for u in range(2):
+                nc.vector.tensor_copy(c_tok[u][:].indirect(entries(list1, run)), tile[:, u, :])
 
         y_tiles = [keep.tile([P, 4, len(run) * C], F32, name=f"y{run.start}") for run in Y_RUNS]
         y = {f: tile[:, :, place(f, run)] for run, tile in zip(Y_RUNS, y_tiles) for f in run}
-        grouped = [keep.tile([P, len(run) * C, 4], BF16, name=f"grouped{run.start}", align_bytes=64) for run in G_RUNS]
-        c_bf = [keep.tile([P, T], BF16, name=f"c_bf{t}")[:] for t in range(2)]
 
-        def gather_scalar(a, t):
-            nc.scalar.activation(grouped[a][:, :, t], c_bf[t].indirect(entries(list2, G_RUNS[a])), ACT.Copy)
-
-        def gather_vector(a, t):
-            nc.vector.tensor_copy(grouped[a][:, :, t], c_tok[t][:].indirect(entries(list2, G_RUNS[a])))
-
-        def experts2(a):
-            run = G_RUNS[a]
+        for run in G_RUNS:
+            grouped = keep.tile([P, len(run) * C, 2], U32, name=f"grouped{run.start}", align_bytes=64)
+            for u in range(2):
+                nc.vector.tensor_copy(grouped[:, :, u], c_tok[u][:].bitcast(U32).indirect(entries(list2, run)))
             codes = keep.tile([P, len(run) * C], U32, name=f"codes{run.start}", align_bytes=64)
             scales = keep.tile([P, len(run) * C], U8, name=f"scales{run.start}", align_bytes=64)
             nc.vector.quantize_mx(
-                out=codes[:].bitcast(FP8X4), scales=scales[:], in_=grouped[a][:].rearrange("p m t -> p (m t)")
+                out=codes[:].bitcast(FP8X4),
+                scales=scales[:],
+                in_=grouped[:].rearrange("p m u -> p (m u)").bitcast(BF16),
             )
             for f in run:
                 for blocks in runs(1, 3) if f == 0 else runs(4):
@@ -192,26 +192,6 @@ def tile_moe_ser_gelu_kernel(
                             stop=True,
                         )
                     nc.scalar.copy(y[f][:, blocks.start : blocks.stop, :], sums[:])
-
-        for t in range(2):
-            nc.scalar.copy(c_bf[t], c_tok[t][:])
-            for a in range(len(G_RUNS)):
-                gather_scalar(a, t)
-        for t in range(2, 4):
-            gather_vector(0, t)
-        experts2(0)
-        late = keep.tile([P, 2, T], BF16, name="grouped0", align_bytes=64)
-        for t in range(2, 4):
-            c_bf.append(late[:, t - 2, :])
-            nc.vector.tensor_copy(c_bf[t], c_tok[t][:])
-        for a in range(1, len(G_RUNS)):
-            for t in range(2, 4):
-                gather_scalar(a, t)
-            if a == 1:
-                experts2(a)
-            if a > 2:
-                experts2(a - 1)
-        experts2(len(G_RUNS) - 1)
 
         out_tok = [keep.tile([P, T], F32, name=f"out_tok{b}") for b in range(4)]
         for run, tile in zip(Y_RUNS, y_tiles):

@@ -27,13 +27,14 @@ def runs(*sizes):
     return [range(a, b) for a, b in zip(edges, edges[1:])]
 
 
-XS_RUNS = runs(4,4)
-XW_RUNS = runs(1,3,4)
-W1_RUNS = runs(1,1,2,4)
-S1_RUNS = runs(2,6)
-C_RUNS = runs(1,1,2,2,2)
-G_RUNS = runs(1,1,2,2,2)
-Y_RUNS = runs(1,1,2,2,2)
+XS_RUNS = runs(2,6)
+W1_RUNS = runs(1,3,2,2)
+S1_RUNS = runs(3,5)
+XW_RUNS = runs(1,1,2,4)
+C_RUNS = runs(1,1,1,1,1,1,2)
+G_RUNS = runs(1,1,1,1,2,2)
+VECTOR_RUNS = 3
+Y_RUNS = runs(1,1,1,1,2,2)
 
 
 def tile_moe_ser_gelu_kernel(
@@ -54,69 +55,65 @@ def tile_moe_ser_gelu_kernel(
         lists = ctx.enter_context(tc.tile_pool(name="lists", bufs=1))
         keep = ctx.enter_context(tc.tile_pool(name="keep", bufs=1))
         ring = ctx.enter_context(tc.tile_pool(name="ring", bufs=3))
-        psum = ctx.enter_context(tc.psum_pool(name="psum", bufs=2))
+        psum = ctx.enter_context(tc.psum_pool(name="psum", bufs=3))
 
         list1 = lists.tile([P, T // 16], U16, name="list1")
         list2 = lists.tile([P, T // 16], U16, name="list2")
         nc.sync.dma_start(list1[:], offs)
 
-        xs = keep.tile([P, T], U8, name="xs", align_bytes=64)
-        nc.gpsimd.memset(xs[:].bitcast(I32), 0)
         warm = keep.tile([P, 16], F32, name="warm")
         nc.gpsimd.memset(warm[:, 0:8], 0.0)
         nc.scalar.activation(warm[:, 8:16], warm[:, 0:8], ACT.Gelu_apprx_tanh)
-        w1s_tiles = [keep.tile([P, 2 * len(run), H], U8, name=f"w1s{run.start}", align_bytes=64) for run in S1_RUNS]
-        nc.vector.memset(w1s_tiles[0][:].rearrange("p a n -> p (a n)").bitcast(I32), 0)
+        xs = keep.tile([P, T], U8, name="xs", align_bytes=64)
+        nc.gpsimd.memset(xs[:].bitcast(I32), 0)
+        ws_first = keep.tile([P, 2 * len(S1_RUNS[0]), H], U8, name="ws_first", align_bytes=64)
+        nc.vector.memset(ws_first[:].rearrange("p a n -> p (a n)").bitcast(I32), 0)
         g1_rows = keep.tile([P, P], F32, name="g1_rows")
         nc.gpsimd.memset(g1_rows[:], 0.0)
+        nc.gpsimd.dma_start(g1_rows[0:E, :], gate1[0:1, :].rearrange("o (e u) -> (o e) u", e=E))
         ident = keep.tile([P, P], F32, name="ident")
         make_identity(nc, ident[:])
-        nc.vector.memset(w1s_tiles[1][:].rearrange("p a n -> p (a n)").bitcast(I32), 0)
-
-        for q in range(2):
-            nc.sync.dma_start(xs[32 * q : 32 * q + 8, :].bitcast(I32), x_scales[:, 4 * q : 4 * q + 4, :].bitcast(I32))
-        for q in range(2, 4):
-            for s in range(2):
-                first = 32 * q - 4 * s
-                nc.sync.dma_start(xs[first : first + 4, :].bitcast(I32), x_scales[s, 4 * q : 4 * q + 4, :].bitcast(I32))
-        xw = keep.tile([P, 2, T], I32, name="xw")
-        nc.sync.dma_start(xw[:], x_words.rearrange("s p t d -> p s (t d)").bitcast(I32))
 
         def load_planes(tile, scales):
             rows = scales.rearrange("e s (q r) n -> r q (e s) n", r=4)
             for r in range(4):
                 nc.sync.dma_start(tile[r:P:32, :, :].bitcast(I32), rows[r].bitcast(I32))
 
+        def load_words(words, name):
+            tile = keep.tile([P, words.shape[0] * words.shape[1], 2 * H], U8, name=name, align_bytes=64)
+            nc.sync.dma_start(tile[:].bitcast(I32), words.rearrange("e s p n -> p (e s) n").bitcast(I32))
+            return tile
+
+        for q in range(4):
+            nc.sync.dma_start(xs[32 * q : 32 * q + 8, :].bitcast(I32), x_scales[:, 4 * q : 4 * q + 4, :].bitcast(I32))
+        nc.sync.dma_start(list2[:], offs2)
+        xw = keep.tile([P, 2, T], I32, name="xw")
+        nc.sync.dma_start(xw[:], x_words.rearrange("s p t d -> p s (t d)").bitcast(I32))
         w1w = {}
-        w1s = {e: tile[:, 2 * (e - run.start) : 2 * (e - run.start) + 2, :] for run, tile in zip(S1_RUNS, w1s_tiles) for e in run}
-        load_planes(w1s_tiles[0], w1_scales[S1_RUNS[0].start : S1_RUNS[0].stop])
-        for run in W1_RUNS:
-            tile = keep.tile([P, 2 * len(run), 2 * H], U8, name=f"w1w{run.start}", align_bytes=64)
-            nc.sync.dma_start(
-                tile[:].bitcast(I32), w1_words[run.start : run.stop].rearrange("e s p n -> p (e s) n").bitcast(I32)
-            )
+
+        def load_w1(run, name):
+            tile = load_words(w1_words[run.start : run.stop], name)
             for e in run:
                 w1w[e] = tile[:, 2 * (e - run.start) : 2 * (e - run.start) + 2, :]
-            if run.stop == 1:
-                nc.sync.dma_start(g1_rows[0:E, :], gate1[0:1, :].rearrange("o (e u) -> (o e) u", e=E))
-            if run.stop == S1_RUNS[1].start:
-                load_planes(w1s_tiles[1], w1_scales[S1_RUNS[1].start : S1_RUNS[1].stop])
-        nc.sync.dma_start(list2[:], offs2)
-        w2w = keep.tile([P, E, 2 * N], U8, name="w2w", align_bytes=64)
-        nc.sync.dma_start(w2w[:].bitcast(I32), w2_words.rearrange("e s p n -> p (e s) n").bitcast(I32))
-        g2 = keep.tile([P, T], F32, name="g2")
-        nc.sync.dma_start(g2[:], gate2)
+
+        load_w1(W1_RUNS[0], "words_a")
+        load_planes(ws_first, w1_scales[S1_RUNS[0].start : S1_RUNS[0].stop])
+        load_w1(W1_RUNS[1], "words_b")
 
         xs_slot = {}
         for run in XS_RUNS:
             gathered = keep.tile([P, len(run) * C], U8, name=f"xs_pass0_{run.start}", align_bytes=64)
             shifted = keep.tile([P, len(run) * C], U8, name=f"xs_pass1_{run.start}", align_bytes=64)
+            nc.vector.memset(shifted[:].bitcast(I32), 0)
             nc.vector.tensor_copy(gathered[:], xs[:].indirect(entries(list1, run)))
-            nc.scalar.dma_start(shifted[0:64, :].bitcast(I32), gathered[4:68, :].bitcast(I32))
-            nc.scalar.dma_start(shifted[64:128, :].bitcast(I32), gathered[60:124, :].bitcast(I32))
+            nc.scalar.dma_start(shifted[0:100, :].bitcast(I32), gathered[4:104, :].bitcast(I32))
             for e in run:
                 xs_slot[e, 0] = gathered[:, place(e, run)]
                 xs_slot[e, 1] = shifted[:, place(e, run)]
+        ws = keep.tile([P, 2 * len(S1_RUNS[1]), H], U8, name="xs", align_bytes=64)
+        nc.gpsimd.memset(ws[:].rearrange("p a n -> p (a n)").bitcast(I32), 0)
+        load_planes(ws, w1_scales[S1_RUNS[1].start : S1_RUNS[1].stop])
+        w1s = {e: tile[:, 2 * (e - run.start) : 2 * (e - run.start) + 2, :] for run, tile in zip(S1_RUNS, [ws_first, ws]) for e in run}
         xw_slot = {}
         for run in XW_RUNS:
             for s in range(2):
@@ -135,7 +132,7 @@ def tile_moe_ser_gelu_kernel(
             tile = keep.tile([P, 2, len(run) * C], F32, name=f"c_slot{run.start}")
             c_slot.append(tile)
             for e in run:
-                sums = psum.tile([P, H], F32, name="sums1", bufs=3)
+                sums = psum.tile([P, H], F32, name="sums1", bufs=2)
                 for s in range(2):
                     nc.tensor.matmul_mx(
                         out=sums[:],
@@ -146,41 +143,70 @@ def tile_moe_ser_gelu_kernel(
                         start=(s == 0),
                         stop=(s == 1),
                     )
-                h = ring.tile([P, 2, P, 2], F32, name="h")
-                nc.scalar.activation(h[:], sums[:].rearrange("m (p u d) -> m u p d", u=2, d=2), ACT.Gelu_apprx_tanh)
-                c_rows = ring.tile([P, H], BF16, name="c_rows")
-                nc.scalar.activation(c_rows[:], h[:].rearrange("m u p d -> m (u p d)"), ACT.Copy, scale=g1[:, e : e + 1])
-                pairs = c_rows[:].bitcast(F32)
-                turned = psum.tile([P, 2, C], F32, name="turned")
-                for u in range(2):
-                    nc.tensor.transpose(turned[:, u, :], pairs[:, P * u : P * (u + 1)], ident[:])
-                nc.scalar.copy(tile[:, :, place(e, run)], turned[:])
+                if e == 0:
+                    load_w1(W1_RUNS[2], "words_a")
+                if e == 1:
+                    load_w1(W1_RUNS[3], "xw_slot1_1")
+                for words in runs(2):
+                    some = slice(words.start, words.stop)
+                    h = ring.tile([P, len(words), P, 2], F32, name="h")
+                    nc.scalar.activation(
+                        h[:], sums[:].rearrange("m (p u d) -> m u p d", u=2, d=2)[:, some], ACT.Gelu_apprx_tanh
+                    )
+                    c_rows = ring.tile([P, len(words) * 2 * P], BF16, name="c_rows")
+                    nc.scalar.activation(
+                        c_rows[:], h[:].rearrange("m u p d -> m (u p d)"), ACT.Copy, scale=g1[:, e : e + 1]
+                    )
+                    pairs = c_rows[:].bitcast(F32)
+                    turned = psum.tile([P, len(words), C], F32, name="turned")
+                    for u in range(len(words)):
+                        nc.tensor.transpose(turned[:, u, :], pairs[:, P * u : P * (u + 1)], ident[:])
+                    nc.scalar.copy(tile[:, some, place(e, run)], turned[:])
 
-        w2s = w1s_tiles[1][:, 0:E, :]
+        g2 = keep.tile([P, T], F32, name="words_a", align_bytes=64)
+        nc.sync.dma_start(g2[:], gate2)
+        w2s = ws[:, 0:E, :]
         load_planes(w2s, w2_scales)
+        w2w = load_words(w2_words, "words_b")
 
         c_tok = [keep.tile([P, T], F32, name=f"c_tok{u}") for u in range(2)]
         for run, tile in zip(C_RUNS, c_slot):
-            for u in range(2):
-                nc.vector.tensor_copy(c_tok[u][:].indirect(entries(list1, run)), tile[:, u, :])
+            for e in run:
+                one = range(e, e + 1)
+                nc.vector.tensor_copy(c_tok[0][:].indirect(entries(list1, one)), tile[:, 0, place(e, run)])
+            nc.vector.tensor_copy(c_tok[1][:].indirect(entries(list1, run)), tile[:, 1, :])
 
         y_tiles = [keep.tile([P, 4, len(run) * C], F32, name=f"y{run.start}") for run in Y_RUNS]
         y = {f: tile[:, :, place(f, run)] for run, tile in zip(Y_RUNS, y_tiles) for f in run}
 
-        for run in G_RUNS:
-            grouped = keep.tile([P, len(run) * C, 2], U32, name=f"grouped{run.start}", align_bytes=64)
+        grouped = [
+            keep.tile([P, len(run) * C, 4], BF16, name=f"grouped{run.start % 2 if a < VECTOR_RUNS else run.start}", align_bytes=64)
+            for a, run in enumerate(G_RUNS)
+        ]
+        c_plane = [keep.tile([P, T], BF16, name=f"c_plane{t}") for t in range(4)]
+
+        def part(t):
+            nc.scalar.copy(c_plane[t][:], c_tok[t // 2][:].bitcast(BF16)[:, t % 2 :: 2])
+
+        def gather_scalar(a, planes):
+            for t in planes:
+                nc.scalar.activation(grouped[a][:, :, t], c_plane[t][:].indirect(entries(list2, G_RUNS[a])), ACT.Copy)
+
+        def gather_vector(a):
+            words = grouped[a][:].rearrange("p m t -> p (m t)").bitcast(U32)
             for u in range(2):
-                nc.vector.tensor_copy(grouped[:, :, u], c_tok[u][:].bitcast(U32).indirect(entries(list2, run)))
+                nc.vector.tensor_copy(words[:, u::2], c_tok[u][:].bitcast(U32).indirect(entries(list2, G_RUNS[a])))
+
+        def experts2(a):
+            run = G_RUNS[a]
             codes = keep.tile([P, len(run) * C], U32, name=f"codes{run.start}", align_bytes=64)
             scales = keep.tile([P, len(run) * C], U8, name=f"scales{run.start}", align_bytes=64)
             nc.vector.quantize_mx(
-                out=codes[:].bitcast(FP8X4),
-                scales=scales[:],
-                in_=grouped[:].rearrange("p m u -> p (m u)").bitcast(BF16),
+                out=codes[:].bitcast(FP8X4), scales=scales[:], in_=grouped[a][:].rearrange("p m t -> p (m t)")
             )
             for f in run:
                 for blocks in runs(1, 3) if f == 0 else runs(4):
-                    sums = psum.tile([P, len(blocks), C], F32, name="sums2", bufs=3)
+                    sums = psum.tile([P, len(blocks), C], F32, name="sums2")
                     for b in blocks:
                         nc.tensor.matmul_mx(
                             out=sums[:, b - blocks.start, :],
@@ -192,6 +218,23 @@ def tile_moe_ser_gelu_kernel(
                             stop=True,
                         )
                     nc.scalar.copy(y[f][:, blocks.start : blocks.stop, :], sums[:])
+
+        gather_vector(0)
+        experts2(0)
+        gather_vector(1)
+        experts2(1)
+        gather_vector(2)
+        part(0)
+        part(1)
+        gather_scalar(3, range(2))
+        part(2)
+        part(3)
+        gather_scalar(3, range(2, 4))
+        experts2(2)
+        for a in range(VECTOR_RUNS, len(G_RUNS)):
+            if a + 1 < len(G_RUNS):
+                gather_scalar(a + 1, range(4))
+            experts2(a)
 
         out_tok = [keep.tile([P, T], F32, name=f"out_tok{b}") for b in range(4)]
         for run, tile in zip(Y_RUNS, y_tiles):

@@ -20,6 +20,7 @@ FP8X4 = mybir.dt.float8_e4m3fn_x4
 FP4X4 = mybir.dt.float4_e2m1fn_x4
 ACT = mybir.ActivationFunctionType
 MULT = mybir.AluOpType.mult
+ADD = mybir.AluOpType.add
 
 
 def runs(*sizes):
@@ -31,10 +32,9 @@ XS_RUNS = runs(2,6)
 W1_RUNS = runs(1,3,2,2)
 S1_RUNS = runs(3,5)
 XW_RUNS = runs(1,1,2,4)
-C_RUNS = runs(1,1,1,1,1,1,2)
-G_RUNS = runs(1,1,1,1,2,2)
-VECTOR_RUNS = 3
-Y_RUNS = runs(1,1,1,1,2,2)
+C_RUNS = runs(1,1,1,1,1,3)
+Y_RUNS = runs(1,1,1,1,1,1,2)
+SHARED = 3
 
 
 def tile_moe_ser_gelu_kernel(
@@ -54,21 +54,20 @@ def tile_moe_ser_gelu_kernel(
     with ExitStack() as ctx:
         lists = ctx.enter_context(tc.tile_pool(name="lists", bufs=1))
         keep = ctx.enter_context(tc.tile_pool(name="keep", bufs=1))
-        ring = ctx.enter_context(tc.tile_pool(name="ring", bufs=3))
         psum = ctx.enter_context(tc.psum_pool(name="psum", bufs=3))
 
         list1 = lists.tile([P, T // 16], U16, name="list1")
         list2 = lists.tile([P, T // 16], U16, name="list2")
         nc.sync.dma_start(list1[:], offs)
 
+        xs = keep.tile([P, T], U8, name="xs", align_bytes=64)
+        nc.gpsimd.memset(xs[:].bitcast(I32), 0)
         warm = keep.tile([P, 16], F32, name="warm")
         nc.gpsimd.memset(warm[:, 0:8], 0.0)
         nc.scalar.activation(warm[:, 8:16], warm[:, 0:8], ACT.Gelu_apprx_tanh)
-        xs = keep.tile([P, T], U8, name="xs", align_bytes=64)
-        nc.gpsimd.memset(xs[:].bitcast(I32), 0)
         ws_first = keep.tile([P, 2 * len(S1_RUNS[0]), H], U8, name="ws_first", align_bytes=64)
         nc.vector.memset(ws_first[:].rearrange("p a n -> p (a n)").bitcast(I32), 0)
-        g1_rows = keep.tile([P, P], F32, name="g1_rows")
+        g1_rows = keep.tile([P, P], F32, name="g1_rows", align_bytes=64)
         nc.gpsimd.memset(g1_rows[:], 0.0)
         nc.gpsimd.dma_start(g1_rows[0:E, :], gate1[0:1, :].rearrange("o (e u) -> (o e) u", e=E))
         ident = keep.tile([P, P], F32, name="ident")
@@ -127,6 +126,11 @@ def tile_moe_ser_gelu_kernel(
         g1 = keep.tile([P, E], F32, name="g1")
         nc.scalar.copy(g1[:], g1_turned[:, 0:E])
 
+        load_w1(W1_RUNS[2], "g1_rows")
+        h_place, c_place = [0, 0], [1, 2, 3]
+        for e in range(2, E):
+            h_place.append(c_place[e - 2])
+            c_place.append(h_place[e - 1])
         c_slot = []
         for run in C_RUNS:
             tile = keep.tile([P, 2, len(run) * C], F32, name=f"c_slot{run.start}")
@@ -144,26 +148,20 @@ def tile_moe_ser_gelu_kernel(
                         stop=(s == 1),
                     )
                 if e == 0:
-                    load_w1(W1_RUNS[2], "words_a")
-                if e == 1:
-                    load_w1(W1_RUNS[3], "xw_slot1_1")
-                for words in runs(2):
-                    some = slice(words.start, words.stop)
-                    h = ring.tile([P, len(words), P, 2], F32, name="h")
-                    nc.scalar.activation(
-                        h[:], sums[:].rearrange("m (p u d) -> m u p d", u=2, d=2)[:, some], ACT.Gelu_apprx_tanh
-                    )
-                    c_rows = ring.tile([P, len(words) * 2 * P], BF16, name="c_rows")
-                    nc.scalar.activation(
-                        c_rows[:], h[:].rearrange("m u p d -> m (u p d)"), ACT.Copy, scale=g1[:, e : e + 1]
-                    )
-                    pairs = c_rows[:].bitcast(F32)
-                    turned = psum.tile([P, len(words), C], F32, name="turned")
-                    for u in range(len(words)):
-                        nc.tensor.transpose(turned[:, u, :], pairs[:, P * u : P * (u + 1)], ident[:])
-                    nc.scalar.copy(tile[:, some, place(e, run)], turned[:])
+                    load_w1(W1_RUNS[3], "words_a")
+                h = keep.tile([P, 2, P, 2], F32, name=f"rows{h_place[e]}")
+                nc.scalar.activation(h[:], sums[:].rearrange("m (p u d) -> m u p d", u=2, d=2), ACT.Gelu_apprx_tanh)
+                c_both = keep.tile([P, 2, 2 * P], BF16, name=f"rows{c_place[e]}")
+                c_rows = [c_both[:, u, :] for u in range(2)]
+                h_rows = [h[:, u].rearrange("m p d -> m (p d)") for u in range(2)]
+                nc.scalar.activation(c_rows[0], h_rows[0], ACT.Copy, scale=g1[:, e : e + 1])
+                nc.gpsimd.tensor_scalar(c_rows[1], h_rows[1], g1[:, e : e + 1], 0.0, MULT, ADD)
+                turned = psum.tile([P, 2, C], F32, name="turned")
+                for u in range(2):
+                    nc.tensor.transpose(turned[:, u, :], c_rows[u].bitcast(F32), ident[:])
+                nc.scalar.copy(tile[:, :, place(e, run)], turned[:])
 
-        g2 = keep.tile([P, T], F32, name="words_a", align_bytes=64)
+        g2 = keep.tile([P, T], F32, name="xw_slot2_1", align_bytes=64)
         nc.sync.dma_start(g2[:], gate2)
         w2s = ws[:, 0:E, :]
         load_planes(w2s, w2_scales)
@@ -171,72 +169,73 @@ def tile_moe_ser_gelu_kernel(
 
         c_tok = [keep.tile([P, T], F32, name=f"c_tok{u}") for u in range(2)]
         for run, tile in zip(C_RUNS, c_slot):
-            for e in run:
-                one = range(e, e + 1)
-                nc.vector.tensor_copy(c_tok[0][:].indirect(entries(list1, one)), tile[:, 0, place(e, run)])
+            for some in [run] if len(run) == 1 else [run[:-1], run[-1:]]:
+                columns = slice((some.start - run.start) * C, (some.stop - run.start) * C)
+                nc.vector.tensor_copy(c_tok[0][:].indirect(entries(list1, some)), tile[:, 0, columns])
             nc.vector.tensor_copy(c_tok[1][:].indirect(entries(list1, run)), tile[:, 1, :])
 
         y_tiles = [keep.tile([P, 4, len(run) * C], F32, name=f"y{run.start}") for run in Y_RUNS]
         y = {f: tile[:, :, place(f, run)] for run, tile in zip(Y_RUNS, y_tiles) for f in run}
-
-        grouped = [
-            keep.tile([P, len(run) * C, 4], BF16, name=f"grouped{run.start % 2 if a < VECTOR_RUNS else run.start}", align_bytes=64)
-            for a, run in enumerate(G_RUNS)
-        ]
-        c_plane = [keep.tile([P, T], BF16, name=f"c_plane{t}") for t in range(4)]
-
-        def part(t):
-            nc.scalar.copy(c_plane[t][:], c_tok[t // 2][:].bitcast(BF16)[:, t % 2 :: 2])
-
-        def gather_scalar(a, planes):
-            for t in planes:
-                nc.scalar.activation(grouped[a][:, :, t], c_plane[t][:].indirect(entries(list2, G_RUNS[a])), ACT.Copy)
-
-        def gather_vector(a):
-            words = grouped[a][:].rearrange("p m t -> p (m t)").bitcast(U32)
-            for u in range(2):
-                nc.vector.tensor_copy(words[:, u::2], c_tok[u][:].bitcast(U32).indirect(entries(list2, G_RUNS[a])))
-
-        def experts2(a):
-            run = G_RUNS[a]
-            codes = keep.tile([P, len(run) * C], U32, name=f"codes{run.start}", align_bytes=64)
-            scales = keep.tile([P, len(run) * C], U8, name=f"scales{run.start}", align_bytes=64)
-            nc.vector.quantize_mx(
-                out=codes[:].bitcast(FP8X4), scales=scales[:], in_=grouped[a][:].rearrange("p m t -> p (m t)")
-            )
-            for f in run:
-                for blocks in runs(1, 3) if f == 0 else runs(4):
-                    sums = psum.tile([P, len(blocks), C], F32, name="sums2")
-                    for b in blocks:
-                        nc.tensor.matmul_mx(
-                            out=sums[:, b - blocks.start, :],
-                            lhsT=w2w[:, f, 2 * P * b : 2 * P * (b + 1)].bitcast(FP4X4),
-                            lhsT_scale=w2s[:, f, P * b : P * (b + 1)],
-                            rhs=codes[:, place(f, run)].bitcast(FP8X4),
-                            rhs_scale=scales[:, place(f, run)],
-                            start=True,
-                            stop=True,
-                        )
-                    nc.scalar.copy(y[f][:, blocks.start : blocks.stop, :], sums[:])
-
-        gather_vector(0)
-        experts2(0)
-        gather_vector(1)
-        experts2(1)
-        gather_vector(2)
-        part(0)
-        part(1)
-        gather_scalar(3, range(2))
-        part(2)
-        part(3)
-        gather_scalar(3, range(2, 4))
-        experts2(2)
-        for a in range(VECTOR_RUNS, len(G_RUNS)):
-            if a + 1 < len(G_RUNS):
-                gather_scalar(a + 1, range(4))
-            experts2(a)
-
         out_tok = [keep.tile([P, T], F32, name=f"out_tok{b}") for b in range(4)]
+        grouped, c_plane, codes, scales = {}, {}, {}, {}
+
+        def halves(t):
+            return c_tok[t // 2][:].bitcast(BF16)[:, t % 2 :: 2]
+
+        def part(t, name):
+            c_plane[t] = keep.tile([P, T], BF16, name=name, align_bytes=64)
+            nc.scalar.copy(c_plane[t][:], halves(t))
+
+        def gather_scalar(f, planes):
+            for t in planes:
+                nc.scalar.activation(grouped[f][:, :, t], c_plane[t][:].indirect(entries(list2, range(f, f + 1))), ACT.Copy)
+
+        def gather_vector(f):
+            words = grouped[f][:].rearrange("p m t -> p (m t)").bitcast(U32)
+            nc.vector.tensor_copy(words[:, 1::2], c_tok[1][:].bitcast(U32).indirect(entries(list2, range(f, f + 1))))
+
+        def quantise(f):
+            codes[f] = keep.tile([P, C], U32, name=f"codes{f}", align_bytes=64)
+            scales[f] = keep.tile([P, C], U8, name=f"scales{f}", align_bytes=64)
+            nc.vector.quantize_mx(
+                out=codes[f][:].bitcast(FP8X4), scales=scales[f][:], in_=grouped[f][:].rearrange("p m t -> p (m t)")
+            )
+
+        def products(f):
+            for blocks in runs(1, 3) if f == 0 else runs(4):
+                sums = psum.tile([P, len(blocks), C], F32, name="sums2")
+                for b in blocks:
+                    nc.tensor.matmul_mx(
+                        out=sums[:, b - blocks.start, :],
+                        lhsT=w2w[:, f, 2 * P * b : 2 * P * (b + 1)].bitcast(FP4X4),
+                        lhsT_scale=w2s[:, f, P * b : P * (b + 1)],
+                        rhs=codes[f][:].bitcast(FP8X4),
+                        rhs_scale=scales[f][:],
+                        start=True,
+                        stop=True,
+                    )
+                nc.scalar.copy(y[f][:, blocks.start : blocks.stop, :], sums[:])
+
+        part(0, "c_plane0")
+        c_plane[1] = keep.tile([P, T], BF16, name="c_plane1", align_bytes=64)
+        nc.gpsimd.tensor_scalar(c_plane[1][:], halves(1), 1.0, 0.0, MULT, ADD)
+        for f in range(SHARED):
+            grouped[f] = keep.tile([P, C, 4], BF16, name=f"grouped{f}", align_bytes=64)
+            gather_scalar(f, range(2))
+            gather_vector(f)
+            quantise(f)
+        products(0)
+        products(1)
+        part(2, "codes0")
+        part(3, "scales0")
+        for f in range(SHARED, E):
+            grouped[f] = keep.tile([P, C, 4], BF16, name=f"codes{f - 2}", align_bytes=64)
+            gather_scalar(f, range(4))
+            quantise(f)
+            if f - 1 < E - 3:
+                products(f - 1)
+        for f in range(E - 3, E):
+            products(f)
         for run, tile in zip(Y_RUNS, y_tiles):
             for b in range(4):
                 nc.vector.tensor_tensor(out_tok[b][:].indirect(entries(list2, run)), tile[:, b, :], g2[:, slots(run)], MULT)

@@ -29,12 +29,14 @@ def runs(*sizes):
 
 
 XS_RUNS = runs(2,6)
-W1_RUNS = runs(1,3,2,2)
+W1_RUNS = runs(1,1,2,2,2)
 S1_RUNS = runs(3,5)
 XW_RUNS = runs(1,1,2,4)
 C_RUNS = runs(1,1,1,1,1,3)
 Y_RUNS = runs(1,1,1,1,1,1,2)
 SHARED = 3
+SUM_BANKS = "abbcbcbc"
+TURN_BANKS = "cadadada"
 
 
 def tile_moe_ser_gelu_kernel(
@@ -54,13 +56,14 @@ def tile_moe_ser_gelu_kernel(
     with ExitStack() as ctx:
         lists = ctx.enter_context(tc.tile_pool(name="lists", bufs=1))
         keep = ctx.enter_context(tc.tile_pool(name="keep", bufs=1))
-        psum = ctx.enter_context(tc.psum_pool(name="psum", bufs=3))
+        psum = ctx.enter_context(tc.psum_pool(name="psum", bufs=1))
+        placed = ctx.enter_context(tc.tile_pool(name="placed", bufs=1))
 
         list1 = lists.tile([P, T // 16], U16, name="list1")
         list2 = lists.tile([P, T // 16], U16, name="list2")
         nc.sync.dma_start(list1[:], offs)
 
-        xs = keep.tile([P, T], U8, name="xs", align_bytes=64)
+        xs = placed.tile([P, T], U8, name="xs", align_bytes=64, offset=4096 - T // 2)
         nc.gpsimd.memset(xs[:].bitcast(I32), 0)
         warm = keep.tile([P, 16], F32, name="warm")
         nc.gpsimd.memset(warm[:, 0:8], 0.0)
@@ -78,8 +81,9 @@ def tile_moe_ser_gelu_kernel(
             for r in range(4):
                 nc.sync.dma_start(tile[r:P:32, :, :].bitcast(I32), rows[r].bitcast(I32))
 
-        def load_words(words, name):
-            tile = keep.tile([P, words.shape[0] * words.shape[1], 2 * H], U8, name=name, align_bytes=64)
+        def load_words(words, name, offset=None):
+            pool = keep if offset is None else placed
+            tile = pool.tile([P, words.shape[0] * words.shape[1], 2 * H], U8, name=name, align_bytes=64, offset=offset)
             nc.sync.dma_start(tile[:].bitcast(I32), words.rearrange("e s p n -> p (e s) n").bitcast(I32))
             return tile
 
@@ -90,8 +94,8 @@ def tile_moe_ser_gelu_kernel(
         nc.sync.dma_start(xw[:], x_words.rearrange("s p t d -> p s (t d)").bitcast(I32))
         w1w = {}
 
-        def load_w1(run, name):
-            tile = load_words(w1_words[run.start : run.stop], name)
+        def load_w1(run, name, offset=None):
+            tile = load_words(w1_words[run.start : run.stop], name, offset)
             for e in run:
                 w1w[e] = tile[:, 2 * (e - run.start) : 2 * (e - run.start) + 2, :]
 
@@ -109,7 +113,8 @@ def tile_moe_ser_gelu_kernel(
             for e in run:
                 xs_slot[e, 0] = gathered[:, place(e, run)]
                 xs_slot[e, 1] = shifted[:, place(e, run)]
-        ws = keep.tile([P, 2 * len(S1_RUNS[1]), H], U8, name="xs", align_bytes=64)
+        load_w1(W1_RUNS[2], "words_c", 0)
+        ws = placed.tile([P, 2 * len(S1_RUNS[1]), H], U8, name="ws", align_bytes=64, offset=4096)
         nc.gpsimd.memset(ws[:].rearrange("p a n -> p (a n)").bitcast(I32), 0)
         load_planes(ws, w1_scales[S1_RUNS[1].start : S1_RUNS[1].stop])
         w1s = {e: tile[:, 2 * (e - run.start) : 2 * (e - run.start) + 2, :] for run, tile in zip(S1_RUNS, [ws_first, ws]) for e in run}
@@ -121,22 +126,18 @@ def tile_moe_ser_gelu_kernel(
                 for e in run:
                     xw_slot[e, s] = tile[:, place(e, run)]
 
-        g1_turned = psum.tile([P, P], F32, name="turned")
+        g1_turned = psum.tile([P, P], F32, name="bank_d")
         nc.tensor.transpose(g1_turned[:], g1_rows[:], ident[:])
         g1 = keep.tile([P, E], F32, name="g1")
         nc.scalar.copy(g1[:], g1_turned[:, 0:E])
 
-        load_w1(W1_RUNS[2], "g1_rows")
-        h_place, c_place = [0, 0], [1, 2, 3]
-        for e in range(2, E):
-            h_place.append(c_place[e - 2])
-            c_place.append(h_place[e - 1])
+        load_w1(W1_RUNS[3], "g1_rows")
         c_slot = []
         for run in C_RUNS:
             tile = keep.tile([P, 2, len(run) * C], F32, name=f"c_slot{run.start}")
             c_slot.append(tile)
             for e in run:
-                sums = psum.tile([P, H], F32, name="sums1", bufs=2)
+                sums = psum.tile([P, H], F32, name="bank_" + SUM_BANKS[e])
                 for s in range(2):
                     nc.tensor.matmul_mx(
                         out=sums[:],
@@ -148,15 +149,17 @@ def tile_moe_ser_gelu_kernel(
                         stop=(s == 1),
                     )
                 if e == 0:
-                    load_w1(W1_RUNS[3], "words_a")
-                h = keep.tile([P, 2, P, 2], F32, name=f"rows{h_place[e]}")
+                    load_w1(W1_RUNS[4], "words_a")
+                h = keep.tile([P, 2, P, 2], F32, name=f"h{max(e, 1)}")
                 nc.scalar.activation(h[:], sums[:].rearrange("m (p u d) -> m u p d", u=2, d=2), ACT.Gelu_apprx_tanh)
-                c_both = keep.tile([P, 2, 2 * P], BF16, name=f"rows{c_place[e]}")
+                c_both = keep.tile([P, 2, 2 * P], BF16, name=f"c_both{e}")
                 c_rows = [c_both[:, u, :] for u in range(2)]
-                h_rows = [h[:, u].rearrange("m p d -> m (p d)") for u in range(2)]
-                nc.scalar.activation(c_rows[0], h_rows[0], ACT.Copy, scale=g1[:, e : e + 1])
-                nc.gpsimd.tensor_scalar(c_rows[1], h_rows[1], g1[:, e : e + 1], 0.0, MULT, ADD)
-                turned = psum.tile([P, 2, C], F32, name="turned")
+                c_all = c_both[:].rearrange("m u i -> m (u i)")
+                h_all = h[:].rearrange("m u p d -> m (u p d)")
+                cut = 2 * P if e < 2 else P
+                nc.scalar.activation(c_all[:, 0:cut], h_all[:, 0:cut], ACT.Copy, scale=g1[:, e : e + 1])
+                nc.gpsimd.tensor_scalar(c_all[:, cut:], h_all[:, cut:], g1[:, e : e + 1], 0.0, MULT, ADD)
+                turned = psum.tile([P, 2, C], F32, name="bank_" + TURN_BANKS[e])
                 for u in range(2):
                     nc.tensor.transpose(turned[:, u, :], c_rows[u].bitcast(F32), ident[:])
                 nc.scalar.copy(tile[:, :, place(e, run)], turned[:])
@@ -203,7 +206,7 @@ def tile_moe_ser_gelu_kernel(
 
         def products(f):
             for blocks in runs(1, 3) if f == 0 else runs(4):
-                sums = psum.tile([P, len(blocks), C], F32, name="sums2")
+                sums = psum.tile([P, len(blocks), C], F32, name="sums2", bufs=3)
                 for b in blocks:
                     nc.tensor.matmul_mx(
                         out=sums[:, b - blocks.start, :],

@@ -32,7 +32,7 @@ XS_RUNS = runs(2,6)
 W1_RUNS = runs(1,1,2,2,2)
 S1_RUNS = runs(3,5)
 XW_RUNS = runs(1,1,2,4)
-C_RUNS = runs(1,1,1,1,1,3)
+C_RUNS = runs(1,1,1,1,1,1,2)
 Y_RUNS = runs(1,1,1,1,1,1,2)
 SHARED = 3
 SUM_BANKS = "abbcbcbc"
@@ -159,10 +159,11 @@ def tile_moe_ser_gelu_kernel(
                 cut = 2 * P if e < 2 else P
                 nc.scalar.activation(c_all[:, 0:cut], h_all[:, 0:cut], ACT.Copy, scale=g1[:, e : e + 1])
                 nc.gpsimd.tensor_scalar(c_all[:, cut:], h_all[:, cut:], g1[:, e : e + 1], 0.0, MULT, ADD)
-                turned = psum.tile([P, 2, C], F32, name="bank_" + TURN_BANKS[e])
+                if e == run.start:
+                    turned = psum.tile([P, 2, len(run) * C], F32, name="bank_" + TURN_BANKS[e])
                 for u in range(2):
-                    nc.tensor.transpose(turned[:, u, :], c_rows[u].bitcast(F32), ident[:])
-                nc.scalar.copy(tile[:, :, place(e, run)], turned[:])
+                    nc.tensor.transpose(turned[:, u, place(e, run)], c_rows[u].bitcast(F32), ident[:])
+            nc.scalar.copy(tile[:], turned[:])
 
         g2 = keep.tile([P, T], F32, name="xw_slot2_1", align_bytes=64)
         nc.sync.dma_start(g2[:], gate2)
@@ -171,16 +172,24 @@ def tile_moe_ser_gelu_kernel(
         w2w = load_words(w2_words, "words_b")
 
         c_tok = [keep.tile([P, T], F32, name=f"c_tok{u}") for u in range(2)]
+        grouped, c_plane, codes, scales = {}, {}, {}, {}
+        for f in range(2):
+            grouped[f] = keep.tile([P, C, 4], BF16, name=f"grouped{f}", align_bytes=64)
+
+        def gather_vector(f, u):
+            words = grouped[f][:].rearrange("p m t -> p (m t)").bitcast(U32)
+            nc.vector.tensor_copy(words[:, u::2], c_tok[u][:].bitcast(U32).indirect(entries(list2, range(f, f + 1))))
+
         for run, tile in zip(C_RUNS, c_slot):
-            for some in [run] if len(run) == 1 else [run[:-1], run[-1:]]:
-                columns = slice((some.start - run.start) * C, (some.stop - run.start) * C)
-                nc.vector.tensor_copy(c_tok[0][:].indirect(entries(list1, some)), tile[:, 0, columns])
-            nc.vector.tensor_copy(c_tok[1][:].indirect(entries(list1, run)), tile[:, 1, :])
+            nc.vector.tensor_copy(c_tok[0][:].indirect(entries(list1, run)), tile[:, 0, :])
+            for e in run:
+                if e == E - 1:
+                    gather_vector(0, 0)
+                nc.vector.tensor_copy(c_tok[1][:].indirect(entries(list1, range(e, e + 1))), tile[:, 1, place(e, run)])
 
         y_tiles = [keep.tile([P, 4, len(run) * C], F32, name=f"y{run.start}") for run in Y_RUNS]
         y = {f: tile[:, :, place(f, run)] for run, tile in zip(Y_RUNS, y_tiles) for f in run}
         out_tok = [keep.tile([P, T], F32, name=f"out_tok{b}") for b in range(4)]
-        grouped, c_plane, codes, scales = {}, {}, {}, {}
 
         def halves(t):
             return c_tok[t // 2][:].bitcast(BF16)[:, t % 2 :: 2]
@@ -193,10 +202,6 @@ def tile_moe_ser_gelu_kernel(
             for t in planes:
                 nc.scalar.activation(grouped[f][:, :, t], c_plane[t][:].indirect(entries(list2, range(f, f + 1))), ACT.Copy)
 
-        def gather_vector(f):
-            words = grouped[f][:].rearrange("p m t -> p (m t)").bitcast(U32)
-            nc.vector.tensor_copy(words[:, 1::2], c_tok[1][:].bitcast(U32).indirect(entries(list2, range(f, f + 1))))
-
         def quantise(f):
             codes[f] = keep.tile([P, C], U32, name=f"codes{f}", align_bytes=64)
             scales[f] = keep.tile([P, C], U8, name=f"scales{f}", align_bytes=64)
@@ -204,41 +209,45 @@ def tile_moe_ser_gelu_kernel(
                 out=codes[f][:].bitcast(FP8X4), scales=scales[f][:], in_=grouped[f][:].rearrange("p m t -> p (m t)")
             )
 
-        def products(f):
-            for blocks in runs(1, 3) if f == 0 else runs(4):
-                sums = psum.tile([P, len(blocks), C], F32, name="sums2", bufs=3)
-                for b in blocks:
-                    nc.tensor.matmul_mx(
-                        out=sums[:, b - blocks.start, :],
-                        lhsT=w2w[:, f, 2 * P * b : 2 * P * (b + 1)].bitcast(FP4X4),
-                        lhsT_scale=w2s[:, f, P * b : P * (b + 1)],
-                        rhs=codes[f][:].bitcast(FP8X4),
-                        rhs_scale=scales[f][:],
-                        start=True,
-                        stop=True,
-                    )
-                nc.scalar.copy(y[f][:, blocks.start : blocks.stop, :], sums[:])
+        def products(f, blocks):
+            sums = psum.tile([P, len(blocks), C], F32, name="sums2", bufs=3)
+            for b in blocks:
+                nc.tensor.matmul_mx(
+                    out=sums[:, b - blocks.start, :],
+                    lhsT=w2w[:, f, 2 * P * b : 2 * P * (b + 1)].bitcast(FP4X4),
+                    lhsT_scale=w2s[:, f, P * b : P * (b + 1)],
+                    rhs=codes[f][:].bitcast(FP8X4),
+                    rhs_scale=scales[f][:],
+                    start=True,
+                    stop=True,
+                )
+            nc.scalar.copy(y[f][:, blocks.start : blocks.stop, :], sums[:])
 
         part(0, "c_plane0")
         c_plane[1] = keep.tile([P, T], BF16, name="c_plane1", align_bytes=64)
         nc.gpsimd.tensor_scalar(c_plane[1][:], halves(1), 1.0, 0.0, MULT, ADD)
-        for f in range(SHARED):
-            grouped[f] = keep.tile([P, C, 4], BF16, name=f"grouped{f}", align_bytes=64)
-            gather_scalar(f, range(2))
-            gather_vector(f)
-            quantise(f)
-        products(0)
-        products(1)
-        part(2, "codes0")
+        gather_vector(0, 1)
+        quantise(0)
+        gather_scalar(1, range(2))
+        gather_vector(1, 1)
+        quantise(1)
+        products(0, range(0, 1))
+        products(0, range(1, 4))
+        products(1, range(0, 2))
+        part(2, "c_plane2")
         part(3, "scales0")
-        for f in range(SHARED, E):
+        for f in range(2, E):
             grouped[f] = keep.tile([P, C, 4], BF16, name=f"codes{f - 2}", align_bytes=64)
             gather_scalar(f, range(4))
             quantise(f)
-            if f - 1 < E - 3:
-                products(f - 1)
+            if f < 4:
+                products(f - 1, range(2, 4))
+            elif f - 1 < E - 3:
+                products(f - 1, range(4))
+            if f == 2:
+                products(f, range(0, 2))
         for f in range(E - 3, E):
-            products(f)
+            products(f, range(4))
         for run, tile in zip(Y_RUNS, y_tiles):
             for b in range(4):
                 nc.vector.tensor_tensor(out_tok[b][:].indirect(entries(list2, run)), tile[:, b, :], g2[:, slots(run)], MULT)

@@ -28,15 +28,16 @@ def runs(*sizes):
     return [range(a, b) for a, b in zip(edges, edges[1:])]
 
 
-XS_RUNS = runs(2,6)
-W1_RUNS = runs(1,1,2,2,2)
-S1_RUNS = runs(3,5)
-XW_RUNS = runs(1,1,2,4)
-C_RUNS = runs(1,1,1,1,1,1,2)
-Y_RUNS = runs(1,1,1,1,1,1,2)
-SHARED = 3
+XS_RUNS = runs(2, 6)
+W1_RUNS = runs(1, 1, 2, 2, 2)
+S1_RUNS = runs(3, 5)
+XW_RUNS = runs(1, 1, 2, 4)
+C_RUNS = runs(1, 1, 1, 1, 1, 1, 2)
 SUM_BANKS = "abbcbcbc"
 TURN_BANKS = "cadadada"
+BY_SCALAR = range(1, 5)
+AHEAD = 3
+SPLIT = 9 * C // 2
 
 
 def tile_moe_ser_gelu_kernel(
@@ -52,6 +53,9 @@ def tile_moe_ser_gelu_kernel(
 
     def place(e, run):
         return slice((e - run.start) * C, (e - run.start + 1) * C)
+
+    def one(e):
+        return range(e, e + 1)
 
     with ExitStack() as ctx:
         lists = ctx.enter_context(tc.tile_pool(name="lists", bufs=1))
@@ -153,7 +157,6 @@ def tile_moe_ser_gelu_kernel(
                 h = keep.tile([P, 2, P, 2], F32, name=f"h{max(e, 1)}")
                 nc.scalar.activation(h[:], sums[:].rearrange("m (p u d) -> m u p d", u=2, d=2), ACT.Gelu_apprx_tanh)
                 c_both = keep.tile([P, 2, 2 * P], BF16, name=f"c_both{e}")
-                c_rows = [c_both[:, u, :] for u in range(2)]
                 c_all = c_both[:].rearrange("m u i -> m (u i)")
                 h_all = h[:].rearrange("m u p d -> m (u p d)")
                 cut = 2 * P if e < 2 else P
@@ -162,7 +165,7 @@ def tile_moe_ser_gelu_kernel(
                 if e == run.start:
                     turned = psum.tile([P, 2, len(run) * C], F32, name="bank_" + TURN_BANKS[e])
                 for u in range(2):
-                    nc.tensor.transpose(turned[:, u, place(e, run)], c_rows[u].bitcast(F32), ident[:])
+                    nc.tensor.transpose(turned[:, u, place(e, run)], c_both[:, u, :].bitcast(F32), ident[:])
             nc.scalar.copy(tile[:], turned[:])
 
         g2 = keep.tile([P, T], F32, name="xw_slot2_1", align_bytes=64)
@@ -172,48 +175,46 @@ def tile_moe_ser_gelu_kernel(
         w2w = load_words(w2_words, "words_b")
 
         c_tok = [keep.tile([P, T], F32, name=f"c_tok{u}") for u in range(2)]
-        grouped, c_plane, codes, scales = {}, {}, {}, {}
-        for f in range(2):
-            grouped[f] = keep.tile([P, C, 4], BF16, name=f"grouped{f}", align_bytes=64)
+        grouped, codes, scales = {}, {}, {}
 
-        def gather_vector(f, u):
+        def gather_pair(f, u):
             words = grouped[f][:].rearrange("p m t -> p (m t)").bitcast(U32)
-            nc.vector.tensor_copy(words[:, u::2], c_tok[u][:].bitcast(U32).indirect(entries(list2, range(f, f + 1))))
+            nc.vector.tensor_copy(words[:, u::2], c_tok[u][:].bitcast(U32).indirect(entries(list2, one(f))))
 
+        grouped[0] = keep.tile([P, C, 4], BF16, name="grouped0", align_bytes=64)
         for run, tile in zip(C_RUNS, c_slot):
             nc.vector.tensor_copy(c_tok[0][:].indirect(entries(list1, run)), tile[:, 0, :])
-            for e in run:
-                if e == E - 1:
-                    gather_vector(0, 0)
-                nc.vector.tensor_copy(c_tok[1][:].indirect(entries(list1, range(e, e + 1))), tile[:, 1, place(e, run)])
+            if run.stop == E:
+                gather_pair(0, 0)
+            nc.vector.tensor_copy(c_tok[1][:].indirect(entries(list1, run)), tile[:, 1, :])
 
-        y_tiles = [keep.tile([P, 4, len(run) * C], F32, name=f"y{run.start}") for run in Y_RUNS]
-        y = {f: tile[:, :, place(f, run)] for run, tile in zip(Y_RUNS, y_tiles) for f in run}
-        out_tok = [keep.tile([P, T], F32, name=f"out_tok{b}") for b in range(4)]
+        c_plane = [keep.tile([P, T], BF16, name=f"c_plane{d}", align_bytes=64) for d in range(2)]
+        nc.scalar.copy(c_plane[0][:], c_tok[0][:].bitcast(BF16)[:, 0::2])
+        nc.gpsimd.tensor_scalar(c_plane[1][:], c_tok[0][:].bitcast(BF16)[:, 1::2], 1.0, 0.0, MULT, ADD)
 
-        def halves(t):
-            return c_tok[t // 2][:].bitcast(BF16)[:, t % 2 :: 2]
+        y = keep.tile([P, 4, T], F32, name="y")
 
-        def part(t, name):
-            c_plane[t] = keep.tile([P, T], BF16, name=name, align_bytes=64)
-            nc.scalar.copy(c_plane[t][:], halves(t))
-
-        def gather_scalar(f, planes):
-            for t in planes:
-                nc.scalar.activation(grouped[f][:, :, t], c_plane[t][:].indirect(entries(list2, range(f, f + 1))), ACT.Copy)
-
-        def quantise(f):
+        def bring(f):
+            if f > 0:
+                name = f"grouped{f}" if f < AHEAD else f"codes{f - AHEAD}"
+                grouped[f] = keep.tile([P, C, 4], BF16, name=name, align_bytes=64)
+                if f in BY_SCALAR:
+                    for d in range(2):
+                        nc.scalar.activation(grouped[f][:, :, d], c_plane[d][:].indirect(entries(list2, one(f))), ACT.Copy)
+                else:
+                    gather_pair(f, 0)
+            gather_pair(f, 1)
             codes[f] = keep.tile([P, C], U32, name=f"codes{f}", align_bytes=64)
             scales[f] = keep.tile([P, C], U8, name=f"scales{f}", align_bytes=64)
             nc.vector.quantize_mx(
                 out=codes[f][:].bitcast(FP8X4), scales=scales[f][:], in_=grouped[f][:].rearrange("p m t -> p (m t)")
             )
 
-        def products(f, blocks):
-            sums = psum.tile([P, len(blocks), C], F32, name="sums2", bufs=3)
-            for b in blocks:
+        def products(f):
+            sums = psum.tile([P, 4, C], F32, name="sums2", bufs=4)
+            for b in range(4):
                 nc.tensor.matmul_mx(
-                    out=sums[:, b - blocks.start, :],
+                    out=sums[:, b, :],
                     lhsT=w2w[:, f, 2 * P * b : 2 * P * (b + 1)].bitcast(FP4X4),
                     lhsT_scale=w2s[:, f, P * b : P * (b + 1)],
                     rhs=codes[f][:].bitcast(FP8X4),
@@ -221,35 +222,44 @@ def tile_moe_ser_gelu_kernel(
                     start=True,
                     stop=True,
                 )
-            nc.scalar.copy(y[f][:, blocks.start : blocks.stop, :], sums[:])
+            nc.vector.tensor_tensor(y[:, :, slots(one(f))], sums[:], g2[:, slots(one(f))].unsqueeze(1).to_broadcast([P, 4, C]), MULT)
 
-        part(0, "c_plane0")
-        c_plane[1] = keep.tile([P, T], BF16, name="c_plane1", align_bytes=64)
-        nc.gpsimd.tensor_scalar(c_plane[1][:], halves(1), 1.0, 0.0, MULT, ADD)
-        gather_vector(0, 1)
-        quantise(0)
-        gather_scalar(1, range(2))
-        gather_vector(1, 1)
-        quantise(1)
-        products(0, range(0, 1))
-        products(0, range(1, 4))
-        products(1, range(0, 2))
-        part(2, "c_plane2")
-        part(3, "scales0")
-        for f in range(2, E):
-            grouped[f] = keep.tile([P, C, 4], BF16, name=f"codes{f - 2}", align_bytes=64)
-            gather_scalar(f, range(4))
-            quantise(f)
-            if f < 4:
-                products(f - 1, range(2, 4))
-            elif f - 1 < E - 3:
-                products(f - 1, range(4))
-            if f == 2:
-                products(f, range(0, 2))
-        for f in range(E - 3, E):
-            products(f, range(4))
-        for run, tile in zip(Y_RUNS, y_tiles):
-            for b in range(4):
-                nc.vector.tensor_tensor(out_tok[b][:].indirect(entries(list2, run)), tile[:, b, :], g2[:, slots(run)], MULT)
-                if run.stop == E:
-                    nc.sync.dma_start(out[P * b : P * (b + 1), :], out_tok[b][:])
+        for f in range(AHEAD):
+            bring(f)
+        for f in range(E):
+            products(f)
+            if f + AHEAD < E:
+                bring(f + AHEAD)
+
+        out_tok = [keep.tile([P, T], F32, name=f"out_tok{b}") for b in range(3)]
+        out_tok.append(keep.tile([P, T], F32, name="xw_slot2_1", align_bytes=64))
+
+        def listed(a, b):
+            return list2[:, a // 16 : b // 16]
+
+        def scatter_scalar(b, lo, hi):
+            nc.scalar.activation(out_tok[b][:].indirect(listed(lo, hi)), y[:, b, lo:hi], ACT.Copy)
+
+        def scatter_vector(b, lo, hi):
+            nc.vector.tensor_copy(out_tok[b][:].indirect(listed(lo, hi)), y[:, b, lo:hi])
+
+        def store(b):
+            nc.sync.dma_start(out[P * b : P * (b + 1), :], out_tok[b][:])
+
+        for f in range(3):
+            scatter_scalar(2, f * C, (f + 1) * C)
+            scatter_scalar(1, f * C, (f + 1) * C)
+        scatter_scalar(2, 3 * C, 5 * C)
+        scatter_scalar(1, 3 * C, SPLIT)
+        scatter_scalar(2, 5 * C, 6 * C)
+        scatter_scalar(3, 0, 3 * C)
+        scatter_scalar(2, 6 * C, T)
+        store(2)
+        scatter_vector(0, 2 * C, T)
+        scatter_vector(1, SPLIT, T)
+        store(1)
+        scatter_vector(0, 0, 2 * C)
+        store(0)
+        scatter_scalar(3, 3 * C, 6 * C)
+        scatter_scalar(3, 6 * C, T)
+        store(3)

@@ -35,9 +35,9 @@ XW_RUNS = runs(1, 1, 2, 4)
 C_RUNS = runs(1, 1, 1, 1, 1, 1, 2)
 SUM_BANKS = "abbcbcbc"
 TURN_BANKS = "cadadada"
-BY_SCALAR = range(1, 5)
-AHEAD = 3
-SPLIT = 9 * C // 2
+Q_RUNS = runs(1, 1, 1, 1, 2, 2)
+BY_SCALAR = (1, 2, 3)
+SPLIT = 11 * C // 4
 
 
 def tile_moe_ser_gelu_kernel(
@@ -177,15 +177,15 @@ def tile_moe_ser_gelu_kernel(
         c_tok = [keep.tile([P, T], F32, name=f"c_tok{u}") for u in range(2)]
         grouped, codes, scales = {}, {}, {}
 
-        def gather_pair(f, u):
-            words = grouped[f][:].rearrange("p m t -> p (m t)").bitcast(U32)
-            nc.vector.tensor_copy(words[:, u::2], c_tok[u][:].bitcast(U32).indirect(entries(list2, one(f))))
+        def gather_pair(run, u):
+            words = grouped[run.start][:].rearrange("p m t -> p (m t)").bitcast(U32)
+            nc.vector.tensor_copy(words[:, u::2], c_tok[u][:].bitcast(U32).indirect(entries(list2, run)))
 
         grouped[0] = keep.tile([P, C, 4], BF16, name="grouped0", align_bytes=64)
         for run, tile in zip(C_RUNS, c_slot):
             nc.vector.tensor_copy(c_tok[0][:].indirect(entries(list1, run)), tile[:, 0, :])
             if run.stop == E:
-                gather_pair(0, 0)
+                gather_pair(Q_RUNS[0], 0)
             nc.vector.tensor_copy(c_tok[1][:].indirect(entries(list1, run)), tile[:, 1, :])
 
         c_plane = [keep.tile([P, T], BF16, name=f"c_plane{d}", align_bytes=64) for d in range(2)]
@@ -194,21 +194,26 @@ def tile_moe_ser_gelu_kernel(
 
         y = keep.tile([P, 4, T], F32, name="y")
 
-        def bring(f):
-            if f > 0:
-                name = f"grouped{f}" if f < AHEAD else f"codes{f - AHEAD}"
-                grouped[f] = keep.tile([P, C, 4], BF16, name=name, align_bytes=64)
-                if f in BY_SCALAR:
-                    for d in range(2):
-                        nc.scalar.activation(grouped[f][:, :, d], c_plane[d][:].indirect(entries(list2, one(f))), ACT.Copy)
-                else:
-                    gather_pair(f, 0)
-            gather_pair(f, 1)
-            codes[f] = keep.tile([P, C], U32, name=f"codes{f}", align_bytes=64)
-            scales[f] = keep.tile([P, C], U8, name=f"scales{f}", align_bytes=64)
+        def bring(i):
+            run = Q_RUNS[i]
+            f = run.start
+            if i > 0:
+                name = {4: "codes0", 5: "codes2"}.get(i, f"grouped{f}")
+                grouped[f] = keep.tile([P, len(run) * C, 4], BF16, name=name, align_bytes=64)
+            if i in BY_SCALAR:
+                for d in range(2):
+                    nc.scalar.activation(grouped[f][:, :, d], c_plane[d][:].indirect(entries(list2, run)), ACT.Copy)
+            elif i > 0:
+                gather_pair(run, 0)
+            gather_pair(run, 1)
+            run_codes = keep.tile([P, len(run) * C], U32, name=f"codes{f}", align_bytes=64)
+            run_scales = keep.tile([P, len(run) * C], U8, name=f"scales{f}", align_bytes=64)
             nc.vector.quantize_mx(
-                out=codes[f][:].bitcast(FP8X4), scales=scales[f][:], in_=grouped[f][:].rearrange("p m t -> p (m t)")
+                out=run_codes[:].bitcast(FP8X4), scales=run_scales[:], in_=grouped[f][:].rearrange("p m t -> p (m t)")
             )
+            for e in run:
+                codes[e] = run_codes[:, place(e, run)]
+                scales[e] = run_scales[:, place(e, run)]
 
         def products(f):
             sums = psum.tile([P, 4, C], F32, name="sums2", bufs=4)
@@ -217,25 +222,27 @@ def tile_moe_ser_gelu_kernel(
                     out=sums[:, b, :],
                     lhsT=w2w[:, f, 2 * P * b : 2 * P * (b + 1)].bitcast(FP4X4),
                     lhsT_scale=w2s[:, f, P * b : P * (b + 1)],
-                    rhs=codes[f][:].bitcast(FP8X4),
-                    rhs_scale=scales[f][:],
+                    rhs=codes[f].bitcast(FP8X4),
+                    rhs_scale=scales[f],
                     start=True,
                     stop=True,
                 )
             nc.vector.tensor_tensor(y[:, :, slots(one(f))], sums[:], g2[:, slots(one(f))].unsqueeze(1).to_broadcast([P, 4, C]), MULT)
 
-        for f in range(AHEAD):
-            bring(f)
-        for f in range(E):
+        for i in range(4):
+            bring(i)
+        products(0)
+        bring(4)
+        products(1)
+        products(2)
+        bring(5)
+        for f in range(3, E):
             products(f)
-            if f + AHEAD < E:
-                bring(f + AHEAD)
 
-        out_tok = [keep.tile([P, T], F32, name=f"out_tok{b}") for b in range(3)]
-        out_tok.append(keep.tile([P, T], F32, name="xw_slot2_1", align_bytes=64))
+        out_tok = [keep.tile([P, T], F32, name=f"out_tok{b}") for b in range(4)]
 
-        def listed(a, b):
-            return list2[:, a // 16 : b // 16]
+        def listed(lo, hi):
+            return list2[:, lo // 16 : hi // 16]
 
         def scatter_scalar(b, lo, hi):
             nc.scalar.activation(out_tok[b][:].indirect(listed(lo, hi)), y[:, b, lo:hi], ACT.Copy)
@@ -243,23 +250,20 @@ def tile_moe_ser_gelu_kernel(
         def scatter_vector(b, lo, hi):
             nc.vector.tensor_copy(out_tok[b][:].indirect(listed(lo, hi)), y[:, b, lo:hi])
 
-        def store(b):
-            nc.sync.dma_start(out[P * b : P * (b + 1), :], out_tok[b][:])
+        def store(queue, b):
+            queue.dma_start(out[P * b : P * (b + 1), :], out_tok[b][:])
 
-        for f in range(3):
-            scatter_scalar(2, f * C, (f + 1) * C)
-            scatter_scalar(1, f * C, (f + 1) * C)
-        scatter_scalar(2, 3 * C, 5 * C)
-        scatter_scalar(1, 3 * C, SPLIT)
-        scatter_scalar(2, 5 * C, 6 * C)
-        scatter_scalar(3, 0, 3 * C)
-        scatter_scalar(2, 6 * C, T)
-        store(2)
-        scatter_vector(0, 2 * C, T)
-        scatter_vector(1, SPLIT, T)
-        store(1)
-        scatter_vector(0, 0, 2 * C)
-        store(0)
-        scatter_scalar(3, 3 * C, 6 * C)
-        scatter_scalar(3, 6 * C, T)
-        store(3)
+        for b in range(4):
+            scatter_scalar(b, 0, C)
+        for b in (2, 3):
+            scatter_scalar(b, C, 2 * C)
+        for b in (0, 1):
+            scatter_scalar(b, C, SPLIT)
+        for b in (2, 3):
+            scatter_scalar(b, 2 * C, 5 * C)
+        for b in (0, 1):
+            scatter_vector(b, SPLIT, T)
+            store(nc.sync, b)
+        for b in (2, 3):
+            scatter_scalar(b, 5 * C, T)
+            store(nc.scalar, b)

@@ -33,11 +33,12 @@ W1_RUNS = runs(1, 1, 2, 2, 2)
 S1_RUNS = runs(3, 5)
 XW_RUNS = runs(1, 1, 2, 4)
 C_RUNS = runs(1, 1, 1, 1, 1, 1, 2)
-SUM_BANKS = "abbcbcbc"
-TURN_BANKS = "cadadada"
+SUM_BANKS = "abbcbaed"
+TURN_BANKS = "cacdbac"
+OUT_BANKS = "fghefghe"
 Q_RUNS = runs(1, 1, 1, 1, 2, 2)
 BY_SCALAR = (1, 2, 3)
-SPLIT = 11 * C // 4
+SPLIT = 5 * C // 2
 
 
 def tile_moe_ser_gelu_kernel(
@@ -136,37 +137,47 @@ def tile_moe_ser_gelu_kernel(
         nc.scalar.copy(g1[:], g1_turned[:, 0:E])
 
         load_w1(W1_RUNS[3], "g1_rows")
-        c_slot = []
-        for run in C_RUNS:
+        c_slot, c_both = [], {}
+
+        def front(e):
+            sums = psum.tile([P, H], F32, name="bank_" + SUM_BANKS[e])
+            for s in range(2):
+                nc.tensor.matmul_mx(
+                    out=sums[:],
+                    lhsT=xw_slot[e, s].bitcast(FP8X4),
+                    lhsT_scale=xs_slot[e, s],
+                    rhs=w1w[e][:, s, :].bitcast(FP4X4),
+                    rhs_scale=w1s[e][:, s, :],
+                    start=(s == 0),
+                    stop=(s == 1),
+                )
+            if e == 0:
+                load_w1(W1_RUNS[4], "words_a")
+            h = keep.tile([P, 2, P, 2], F32, name=f"h{max(e, 1)}")
+            nc.scalar.activation(h[:], sums[:].rearrange("m (p u d) -> m u p d", u=2, d=2), ACT.Gelu_apprx_tanh)
+            c_both[e] = keep.tile([P, 2, 2 * P], BF16, name=f"c_both{e}")
+            c_all = c_both[e][:].rearrange("m u i -> m (u i)")
+            h_all = h[:].rearrange("m u p d -> m (u p d)")
+            cut = 2 * P if e < 2 else P
+            nc.scalar.activation(c_all[:, 0:cut], h_all[:, 0:cut], ACT.Copy, scale=g1[:, e : e + 1])
+            nc.gpsimd.tensor_scalar(c_all[:, cut:], h_all[:, cut:], g1[:, e : e + 1], 0.0, MULT, ADD)
+
+        def back(run):
             tile = keep.tile([P, 2, len(run) * C], F32, name=f"c_slot{run.start}")
             c_slot.append(tile)
+            turned = psum.tile([P, 2, len(run) * C], F32, name="bank_" + TURN_BANKS[run.start])
             for e in run:
-                sums = psum.tile([P, H], F32, name="bank_" + SUM_BANKS[e])
-                for s in range(2):
-                    nc.tensor.matmul_mx(
-                        out=sums[:],
-                        lhsT=xw_slot[e, s].bitcast(FP8X4),
-                        lhsT_scale=xs_slot[e, s],
-                        rhs=w1w[e][:, s, :].bitcast(FP4X4),
-                        rhs_scale=w1s[e][:, s, :],
-                        start=(s == 0),
-                        stop=(s == 1),
-                    )
-                if e == 0:
-                    load_w1(W1_RUNS[4], "words_a")
-                h = keep.tile([P, 2, P, 2], F32, name=f"h{max(e, 1)}")
-                nc.scalar.activation(h[:], sums[:].rearrange("m (p u d) -> m u p d", u=2, d=2), ACT.Gelu_apprx_tanh)
-                c_both = keep.tile([P, 2, 2 * P], BF16, name=f"c_both{e}")
-                c_all = c_both[:].rearrange("m u i -> m (u i)")
-                h_all = h[:].rearrange("m u p d -> m (u p d)")
-                cut = 2 * P if e < 2 else P
-                nc.scalar.activation(c_all[:, 0:cut], h_all[:, 0:cut], ACT.Copy, scale=g1[:, e : e + 1])
-                nc.gpsimd.tensor_scalar(c_all[:, cut:], h_all[:, cut:], g1[:, e : e + 1], 0.0, MULT, ADD)
-                if e == run.start:
-                    turned = psum.tile([P, 2, len(run) * C], F32, name="bank_" + TURN_BANKS[e])
                 for u in range(2):
-                    nc.tensor.transpose(turned[:, u, place(e, run)], c_both[:, u, :].bitcast(F32), ident[:])
+                    nc.tensor.transpose(turned[:, u, place(e, run)], c_both[e][:, u, :].bitcast(F32), ident[:])
             nc.scalar.copy(tile[:], turned[:])
+
+        for e in range(E):
+            front(e)
+            if e < 2:
+                back(C_RUNS[e])
+            elif 2 < e < E - 1:
+                back(C_RUNS[e - 1])
+        back(C_RUNS[-1])
 
         g2 = keep.tile([P, T], F32, name="xw_slot2_1", align_bytes=64)
         nc.sync.dma_start(g2[:], gate2)
@@ -216,7 +227,7 @@ def tile_moe_ser_gelu_kernel(
                 scales[e] = run_scales[:, place(e, run)]
 
         def products(f):
-            sums = psum.tile([P, 4, C], F32, name="sums2", bufs=4)
+            sums = psum.tile([P, 4, C], F32, name="bank_" + OUT_BANKS[f])
             for b in range(4):
                 nc.tensor.matmul_mx(
                     out=sums[:, b, :],

@@ -33,12 +33,12 @@ W1_RUNS = runs(1, 1, 2, 2, 2)
 S1_RUNS = runs(3, 5)
 XW_RUNS = runs(1, 1, 2, 4)
 C_RUNS = runs(1, 1, 1, 1, 1, 1, 2)
-SUM_BANKS = "abbcbaed"
+SUM_BANKS = "abfcbaed"
 TURN_BANKS = "cacdbac"
 OUT_BANKS = "fghefghe"
-Q_RUNS = runs(1, 1, 1, 1, 2, 2)
-BY_SCALAR = (1, 2, 3)
-SPLIT = 5 * C // 2
+Q_RUNS = runs(1, 2, 2, 1, 2)
+SHARED = range(1, 5)
+SPLITS = (11 * C // 4, 5 * C // 2)
 
 
 def tile_moe_ser_gelu_kernel(
@@ -62,13 +62,12 @@ def tile_moe_ser_gelu_kernel(
         lists = ctx.enter_context(tc.tile_pool(name="lists", bufs=1))
         keep = ctx.enter_context(tc.tile_pool(name="keep", bufs=1))
         psum = ctx.enter_context(tc.psum_pool(name="psum", bufs=1))
-        placed = ctx.enter_context(tc.tile_pool(name="placed", bufs=1))
 
         list1 = lists.tile([P, T // 16], U16, name="list1")
         list2 = lists.tile([P, T // 16], U16, name="list2")
         nc.sync.dma_start(list1[:], offs)
 
-        xs = placed.tile([P, T], U8, name="xs", align_bytes=64, offset=4096 - T // 2)
+        xs = keep.tile([P, T], U8, name="xs", align_bytes=64)
         nc.gpsimd.memset(xs[:].bitcast(I32), 0)
         warm = keep.tile([P, 16], F32, name="warm")
         nc.gpsimd.memset(warm[:, 0:8], 0.0)
@@ -80,15 +79,16 @@ def tile_moe_ser_gelu_kernel(
         nc.gpsimd.dma_start(g1_rows[0:E, :], gate1[0:1, :].rearrange("o (e u) -> (o e) u", e=E))
         ident = keep.tile([P, P], F32, name="ident")
         make_identity(nc, ident[:])
+        ws = keep.tile([P, 2 * len(S1_RUNS[1]), H], U8, name="ws", align_bytes=64)
+        nc.gpsimd.memset(ws[:].rearrange("p a n -> p (a n)").bitcast(I32), 0)
 
         def load_planes(tile, scales):
             rows = scales.rearrange("e s (q r) n -> r q (e s) n", r=4)
             for r in range(4):
                 nc.sync.dma_start(tile[r:P:32, :, :].bitcast(I32), rows[r].bitcast(I32))
 
-        def load_words(words, name, offset=None):
-            pool = keep if offset is None else placed
-            tile = pool.tile([P, words.shape[0] * words.shape[1], 2 * H], U8, name=name, align_bytes=64, offset=offset)
+        def load_words(words, name):
+            tile = keep.tile([P, words.shape[0] * words.shape[1], 2 * H], U8, name=name, align_bytes=64)
             nc.sync.dma_start(tile[:].bitcast(I32), words.rearrange("e s p n -> p (e s) n").bitcast(I32))
             return tile
 
@@ -99,8 +99,8 @@ def tile_moe_ser_gelu_kernel(
         nc.sync.dma_start(xw[:], x_words.rearrange("s p t d -> p s (t d)").bitcast(I32))
         w1w = {}
 
-        def load_w1(run, name, offset=None):
-            tile = load_words(w1_words[run.start : run.stop], name, offset)
+        def load_w1(run, name):
+            tile = load_words(w1_words[run.start : run.stop], name)
             for e in run:
                 w1w[e] = tile[:, 2 * (e - run.start) : 2 * (e - run.start) + 2, :]
 
@@ -118,9 +118,7 @@ def tile_moe_ser_gelu_kernel(
             for e in run:
                 xs_slot[e, 0] = gathered[:, place(e, run)]
                 xs_slot[e, 1] = shifted[:, place(e, run)]
-        load_w1(W1_RUNS[2], "words_c", 0)
-        ws = placed.tile([P, 2 * len(S1_RUNS[1]), H], U8, name="ws", align_bytes=64, offset=4096)
-        nc.gpsimd.memset(ws[:].rearrange("p a n -> p (a n)").bitcast(I32), 0)
+        load_w1(W1_RUNS[2], "words_c")
         load_planes(ws, w1_scales[S1_RUNS[1].start : S1_RUNS[1].stop])
         w1s = {e: tile[:, 2 * (e - run.start) : 2 * (e - run.start) + 2, :] for run, tile in zip(S1_RUNS, [ws_first, ws]) for e in run}
         xw_slot = {}
@@ -153,18 +151,32 @@ def tile_moe_ser_gelu_kernel(
                 )
             if e == 0:
                 load_w1(W1_RUNS[4], "words_a")
-            h = keep.tile([P, 2, P, 2], F32, name=f"h{max(e, 1)}")
-            nc.scalar.activation(h[:], sums[:].rearrange("m (p u d) -> m u p d", u=2, d=2), ACT.Gelu_apprx_tanh)
+            h = keep.tile([P, 2, P, 2], F32, name=f"h{e}")
+            by_pair = sums[:].rearrange("m (p u d) -> m u p d", u=2, d=2)
             c_both[e] = keep.tile([P, 2, 2 * P], BF16, name=f"c_both{e}")
             c_all = c_both[e][:].rearrange("m u i -> m (u i)")
             h_all = h[:].rearrange("m u p d -> m (u p d)")
-            cut = 2 * P if e < 2 else P
-            nc.scalar.activation(c_all[:, 0:cut], h_all[:, 0:cut], ACT.Copy, scale=g1[:, e : e + 1])
-            nc.gpsimd.tensor_scalar(c_all[:, cut:], h_all[:, cut:], g1[:, e : e + 1], 0.0, MULT, ADD)
+            gate = g1[:, e : e + 1]
+            if e == 0:
+                for u in range(2):
+                    nc.scalar.activation(h[:, u], by_pair[:, u], ACT.Gelu_apprx_tanh)
+                nc.gpsimd.tensor_scalar(c_all[:, 0 : 2 * P], h_all[:, 0 : 2 * P], gate, 0.0, MULT, ADD)
+                nc.scalar.activation(c_all[:, 2 * P :], h_all[:, 2 * P :], ACT.Copy, scale=gate)
+            else:
+                nc.scalar.activation(h[:], by_pair, ACT.Gelu_apprx_tanh)
+                cut = 2 * P if e < 2 else P
+                nc.scalar.activation(c_all[:, 0:cut], h_all[:, 0:cut], ACT.Copy, scale=gate)
+                nc.gpsimd.tensor_scalar(c_all[:, cut:], h_all[:, cut:], gate, 0.0, MULT, ADD)
 
         def back(run):
             tile = keep.tile([P, 2, len(run) * C], F32, name=f"c_slot{run.start}")
             c_slot.append(tile)
+            if run.start == 0:
+                for u, bank in enumerate(["bank_c", "bank_e"]):
+                    half = psum.tile([P, C], F32, name=bank)
+                    nc.tensor.transpose(half[:], c_both[0][:, u, :].bitcast(F32), ident[:])
+                    nc.scalar.copy(tile[:, u, :], half[:])
+                return
             turned = psum.tile([P, 2, len(run) * C], F32, name="bank_" + TURN_BANKS[run.start])
             for e in run:
                 for u in range(2):
@@ -186,17 +198,18 @@ def tile_moe_ser_gelu_kernel(
         w2w = load_words(w2_words, "words_b")
 
         c_tok = [keep.tile([P, T], F32, name=f"c_tok{u}") for u in range(2)]
-        grouped, codes, scales = {}, {}, {}
+        codes, scales = {}, {}
+        wide = len(SHARED) * C
+        dense1 = keep.tile([P, 2 * wide], U32, name="dense1", align_bytes=64)
+        first = dense1[:, wide : wide + 2 * C]
 
-        def gather_pair(run, u):
-            words = grouped[run.start][:].rearrange("p m t -> p (m t)").bitcast(U32)
-            nc.vector.tensor_copy(words[:, u::2], c_tok[u][:].bitcast(U32).indirect(entries(list2, run)))
+        def gather(words, run, u):
+            nc.vector.tensor_copy(words, c_tok[u][:].bitcast(U32).indirect(entries(list2, run)))
 
-        grouped[0] = keep.tile([P, C, 4], BF16, name="grouped0", align_bytes=64)
         for run, tile in zip(C_RUNS, c_slot):
             nc.vector.tensor_copy(c_tok[0][:].indirect(entries(list1, run)), tile[:, 0, :])
             if run.stop == E:
-                gather_pair(Q_RUNS[0], 0)
+                gather(first[:, 0::2], Q_RUNS[0], 0)
             nc.vector.tensor_copy(c_tok[1][:].indirect(entries(list1, run)), tile[:, 1, :])
 
         c_plane = [keep.tile([P, T], BF16, name=f"c_plane{d}", align_bytes=64) for d in range(2)]
@@ -205,26 +218,28 @@ def tile_moe_ser_gelu_kernel(
 
         y = keep.tile([P, 4, T], F32, name="y")
 
-        def bring(i):
-            run = Q_RUNS[i]
-            f = run.start
-            if i > 0:
-                name = {4: "codes0", 5: "codes2"}.get(i, f"grouped{f}")
-                grouped[f] = keep.tile([P, len(run) * C, 4], BF16, name=name, align_bytes=64)
-            if i in BY_SCALAR:
-                for d in range(2):
-                    nc.scalar.activation(grouped[f][:, :, d], c_plane[d][:].indirect(entries(list2, run)), ACT.Copy)
-            elif i > 0:
-                gather_pair(run, 0)
-            gather_pair(run, 1)
-            run_codes = keep.tile([P, len(run) * C], U32, name=f"codes{f}", align_bytes=64)
-            run_scales = keep.tile([P, len(run) * C], U8, name=f"scales{f}", align_bytes=64)
-            nc.vector.quantize_mx(
-                out=run_codes[:].bitcast(FP8X4), scales=run_scales[:], in_=grouped[f][:].rearrange("p m t -> p (m t)")
-            )
+        def quantise(run, grouped):
+            run_codes = keep.tile([P, len(run) * C], U32, name=f"codes{run.start}", align_bytes=64)
+            run_scales = keep.tile([P, len(run) * C], U8, name=f"scales{run.start}", align_bytes=64)
+            nc.vector.quantize_mx(out=run_codes[:].bitcast(FP8X4), scales=run_scales[:], in_=grouped)
             for e in run:
                 codes[e] = run_codes[:, place(e, run)]
                 scales[e] = run_scales[:, place(e, run)]
+
+        def weave(run, name):
+            woven = keep.tile([P, 2 * len(run) * C], F32, name=name, align_bytes=64)
+            fours = slice((run.start - SHARED.start) * C // 4, (run.stop - SHARED.start) * C // 4)
+            nc.vector.tensor_copy(
+                woven[:].rearrange("p (c i u) -> p c u i", i=4, u=2),
+                dense1[:].bitcast(F32).rearrange("p (u c i) -> p c u i", i=4, u=2)[:, fours],
+            )
+            quantise(run, woven[:].bitcast(BF16))
+
+        def bring(run, name):
+            words = keep.tile([P, 2 * len(run) * C], U32, name=name, align_bytes=64)
+            for u in range(2):
+                gather(words[:, u::2], run, u)
+            quantise(run, words[:].bitcast(BF16))
 
         def products(f):
             sums = psum.tile([P, 4, C], F32, name="bank_" + OUT_BANKS[f])
@@ -240,13 +255,18 @@ def tile_moe_ser_gelu_kernel(
                 )
             nc.vector.tensor_tensor(y[:, :, slots(one(f))], sums[:], g2[:, slots(one(f))].unsqueeze(1).to_broadcast([P, 4, C]), MULT)
 
-        for i in range(4):
-            bring(i)
+        gather(first[:, 1::2], Q_RUNS[0], 1)
+        quantise(Q_RUNS[0], first.bitcast(BF16))
+        for d in range(2):
+            nc.scalar.activation(dense1[:, 0:wide].bitcast(BF16)[:, d::2], c_plane[d][:].indirect(entries(list2, SHARED)), ACT.Copy)
+        gather(dense1[:, wide:], SHARED, 1)
         products(0)
-        bring(4)
+        weave(Q_RUNS[1], "codes0")
+        weave(Q_RUNS[2], "scales0")
+        bring(Q_RUNS[3], "codes0")
         products(1)
         products(2)
-        bring(5)
+        bring(Q_RUNS[4], "codes1")
         for f in range(3, E):
             products(f)
 
@@ -269,11 +289,11 @@ def tile_moe_ser_gelu_kernel(
         for b in (2, 3):
             scatter_scalar(b, C, 2 * C)
         for b in (0, 1):
-            scatter_scalar(b, C, SPLIT)
+            scatter_scalar(b, C, SPLITS[b])
         for b in (2, 3):
             scatter_scalar(b, 2 * C, 5 * C)
         for b in (0, 1):
-            scatter_vector(b, SPLIT, T)
+            scatter_vector(b, SPLITS[b], T)
             store(nc.sync, b)
         for b in (2, 3):
             scatter_scalar(b, 5 * C, T)

@@ -32,13 +32,14 @@ XS_RUNS = runs(2, 6)
 W1_RUNS = runs(1, 1, 2, 2, 2)
 S1_RUNS = runs(3, 5)
 XW_RUNS = runs(1, 1, 2, 4)
-C_RUNS = runs(1, 1, 1, 1, 1, 1, 2)
+PUT_RUNS = runs(1, 1, 1, 1, 1, 3)
+PART = 5 * T // 8
 SUM_BANKS = "abfcbaed"
-TURN_BANKS = "cacdbac"
+TURN_BANKS = "cacdbacb"
 OUT_BANKS = "fghefghe"
 Q_RUNS = runs(1, 2, 2, 1, 2)
 SHARED = range(1, 5)
-SPLITS = (11 * C // 4, 5 * C // 2)
+SPLITS = (3 * C, 11 * C // 4)
 
 
 def tile_moe_ser_gelu_kernel(
@@ -73,7 +74,7 @@ def tile_moe_ser_gelu_kernel(
         nc.gpsimd.memset(warm[:, 0:8], 0.0)
         nc.scalar.activation(warm[:, 8:16], warm[:, 0:8], ACT.Gelu_apprx_tanh)
         ws_first = keep.tile([P, 2 * len(S1_RUNS[0]), H], U8, name="ws_first", align_bytes=64)
-        nc.vector.memset(ws_first[:].rearrange("p a n -> p (a n)").bitcast(I32), 0)
+        nc.gpsimd.memset(ws_first[:].rearrange("p a n -> p (a n)").bitcast(I32), 0)
         g1_rows = keep.tile([P, P], F32, name="g1_rows", align_bytes=64)
         nc.gpsimd.memset(g1_rows[:], 0.0)
         nc.gpsimd.dma_start(g1_rows[0:E, :], gate1[0:1, :].rearrange("o (e u) -> (o e) u", e=E))
@@ -135,7 +136,8 @@ def tile_moe_ser_gelu_kernel(
         nc.scalar.copy(g1[:], g1_turned[:, 0:E])
 
         load_w1(W1_RUNS[3], "g1_rows")
-        c_slot, c_both = [], {}
+        c_slot = keep.tile([P, 2, T], F32, name="c_slot")
+        c_both = {}
 
         def front(e):
             sums = psum.tile([P, H], F32, name="bank_" + SUM_BANKS[e])
@@ -164,32 +166,29 @@ def tile_moe_ser_gelu_kernel(
                 nc.scalar.activation(c_all[:, 2 * P :], h_all[:, 2 * P :], ACT.Copy, scale=gate)
             else:
                 nc.scalar.activation(h[:], by_pair, ACT.Gelu_apprx_tanh)
-                cut = 2 * P if e < 2 else P
+                cut = 2 * P if e < 2 or e == E - 1 else P
                 nc.scalar.activation(c_all[:, 0:cut], h_all[:, 0:cut], ACT.Copy, scale=gate)
                 nc.gpsimd.tensor_scalar(c_all[:, cut:], h_all[:, cut:], gate, 0.0, MULT, ADD)
 
-        def back(run):
-            tile = keep.tile([P, 2, len(run) * C], F32, name=f"c_slot{run.start}")
-            c_slot.append(tile)
-            if run.start == 0:
+        def back(e):
+            if e == 0:
                 for u, bank in enumerate(["bank_c", "bank_e"]):
                     half = psum.tile([P, C], F32, name=bank)
                     nc.tensor.transpose(half[:], c_both[0][:, u, :].bitcast(F32), ident[:])
-                    nc.scalar.copy(tile[:, u, :], half[:])
+                    nc.scalar.copy(c_slot[:, u, 0:C], half[:])
                 return
-            turned = psum.tile([P, 2, len(run) * C], F32, name="bank_" + TURN_BANKS[run.start])
-            for e in run:
-                for u in range(2):
-                    nc.tensor.transpose(turned[:, u, place(e, run)], c_both[e][:, u, :].bitcast(F32), ident[:])
-            nc.scalar.copy(tile[:], turned[:])
+            turned = psum.tile([P, 2, C], F32, name="bank_" + TURN_BANKS[e])
+            for u in range(2):
+                nc.tensor.transpose(turned[:, u, :], c_both[e][:, u, :].bitcast(F32), ident[:])
+            nc.scalar.copy(c_slot[:, :, slots(one(e))], turned[:])
 
         for e in range(E):
             front(e)
             if e < 2:
-                back(C_RUNS[e])
-            elif 2 < e < E - 1:
-                back(C_RUNS[e - 1])
-        back(C_RUNS[-1])
+                back(e)
+            elif e > 2:
+                back(e - 1)
+        back(E - 1)
 
         g2 = keep.tile([P, T], F32, name="xw_slot2_1", align_bytes=64)
         nc.sync.dma_start(g2[:], gate2)
@@ -206,15 +205,14 @@ def tile_moe_ser_gelu_kernel(
         def gather(words, run, u):
             nc.vector.tensor_copy(words, c_tok[u][:].bitcast(U32).indirect(entries(list2, run)))
 
-        for run, tile in zip(C_RUNS, c_slot):
-            nc.vector.tensor_copy(c_tok[0][:].indirect(entries(list1, run)), tile[:, 0, :])
-            if run.stop == E:
-                gather(first[:, 0::2], Q_RUNS[0], 0)
-            nc.vector.tensor_copy(c_tok[1][:].indirect(entries(list1, run)), tile[:, 1, :])
+        for run in PUT_RUNS:
+            for u in range(2):
+                nc.vector.tensor_copy(c_tok[u][:].indirect(entries(list1, run)), c_slot[:, u, slots(run)])
 
-        c_plane = [keep.tile([P, T], BF16, name=f"c_plane{d}", align_bytes=64) for d in range(2)]
-        nc.scalar.copy(c_plane[0][:], c_tok[0][:].bitcast(BF16)[:, 0::2])
-        nc.gpsimd.tensor_scalar(c_plane[1][:], c_tok[0][:].bitcast(BF16)[:, 1::2], 1.0, 0.0, MULT, ADD)
+        c_plane = keep.tile([P, 2, T], BF16, name="c_plane", align_bytes=64)
+        halves = c_tok[0][:].bitcast(BF16).rearrange("p (t d) -> p d t", d=2)
+        nc.scalar.copy(c_plane[:, :, 0:PART], halves[:, :, 0:PART])
+        nc.gpsimd.tensor_scalar(c_plane[:, :, PART:], halves[:, :, PART:], 1.0, 0.0, MULT, ADD)
 
         y = keep.tile([P, 4, T], F32, name="y")
 
@@ -241,11 +239,11 @@ def tile_moe_ser_gelu_kernel(
                 gather(words[:, u::2], run, u)
             quantise(run, words[:].bitcast(BF16))
 
-        def products(f):
-            sums = psum.tile([P, 4, C], F32, name="bank_" + OUT_BANKS[f])
-            for b in range(4):
+        def products(f, blocks, bank):
+            sums = psum.tile([P, len(blocks), C], F32, name="bank_" + bank)
+            for b in blocks:
                 nc.tensor.matmul_mx(
-                    out=sums[:, b, :],
+                    out=sums[:, b - blocks.start, :],
                     lhsT=w2w[:, f, 2 * P * b : 2 * P * (b + 1)].bitcast(FP4X4),
                     lhsT_scale=w2s[:, f, P * b : P * (b + 1)],
                     rhs=codes[f].bitcast(FP8X4),
@@ -253,22 +251,26 @@ def tile_moe_ser_gelu_kernel(
                     start=True,
                     stop=True,
                 )
-            nc.vector.tensor_tensor(y[:, :, slots(one(f))], sums[:], g2[:, slots(one(f))].unsqueeze(1).to_broadcast([P, 4, C]), MULT)
+            gate = g2[:, slots(one(f))].unsqueeze(1).to_broadcast([P, len(blocks), C])
+            nc.vector.tensor_tensor(y[:, blocks.start : blocks.stop, slots(one(f))], sums[:], gate, MULT)
 
+        for d in range(2):
+            nc.scalar.activation(first.bitcast(BF16)[:, d::4], c_plane[:, d, :].indirect(entries(list2, Q_RUNS[0])), ACT.Copy)
         gather(first[:, 1::2], Q_RUNS[0], 1)
         quantise(Q_RUNS[0], first.bitcast(BF16))
         for d in range(2):
-            nc.scalar.activation(dense1[:, 0:wide].bitcast(BF16)[:, d::2], c_plane[d][:].indirect(entries(list2, SHARED)), ACT.Copy)
+            nc.scalar.activation(dense1[:, 0:wide].bitcast(BF16)[:, d::2], c_plane[:, d, :].indirect(entries(list2, SHARED)), ACT.Copy)
         gather(dense1[:, wide:], SHARED, 1)
-        products(0)
+        products(0, range(0, 1), "a")
+        products(0, range(1, 4), OUT_BANKS[0])
         weave(Q_RUNS[1], "codes0")
         weave(Q_RUNS[2], "scales0")
         bring(Q_RUNS[3], "codes0")
-        products(1)
-        products(2)
+        products(1, range(4), OUT_BANKS[1])
+        products(2, range(4), OUT_BANKS[2])
         bring(Q_RUNS[4], "codes1")
         for f in range(3, E):
-            products(f)
+            products(f, range(4), OUT_BANKS[f])
 
         out_tok = [keep.tile([P, T], F32, name=f"out_tok{b}") for b in range(4)]
 

@@ -70,9 +70,6 @@ def tile_moe_ser_gelu_kernel(
 
         xs = keep.tile([P, T], U8, name="xs", align_bytes=64)
         nc.gpsimd.memset(xs[:].bitcast(I32), 0)
-        warm = keep.tile([P, 16], F32, name="warm")
-        nc.gpsimd.memset(warm[:, 0:8], 0.0)
-        nc.scalar.activation(warm[:, 8:16], warm[:, 0:8], ACT.Gelu_apprx_tanh)
         ws_first = keep.tile([P, 2 * len(S1_RUNS[0]), H], U8, name="ws_first", align_bytes=64)
         nc.gpsimd.memset(ws_first[:].rearrange("p a n -> p (a n)").bitcast(I32), 0)
         g1_rows = keep.tile([P, P], F32, name="g1_rows", align_bytes=64)

@@ -39,7 +39,7 @@ TURN_BANKS = "cacdbacb"
 OUT_BANKS = "fghefghe"
 Q_RUNS = runs(1, 2, 2, 1, 2)
 SHARED = range(1, 5)
-SPLITS = (3 * C, 11 * C // 4)
+SPLITS = (3 * C, 3 * C)
 
 
 def tile_moe_ser_gelu_kernel(
@@ -248,8 +248,10 @@ def tile_moe_ser_gelu_kernel(
                     start=True,
                     stop=True,
                 )
-            gate = g2[:, slots(one(f))].unsqueeze(1).to_broadcast([P, len(blocks), C])
-            nc.vector.tensor_tensor(y[:, blocks.start : blocks.stop, slots(one(f))], sums[:], gate, MULT)
+            for part in (range(0, 2), range(2, 4)) if f == E - 1 else (blocks,):
+                gate = g2[:, slots(one(f))].unsqueeze(1).to_broadcast([P, len(part), C])
+                part_sums = sums[:, part.start - blocks.start : part.stop - blocks.start, :]
+                nc.vector.tensor_tensor(y[:, part.start : part.stop, slots(one(f))], part_sums, gate, MULT)
 
         for d in range(2):
             nc.scalar.activation(first.bitcast(BF16)[:, d::4], c_plane[:, d, :].indirect(entries(list2, Q_RUNS[0])), ACT.Copy)

from contextlib import ExitStack

import concourse.mybir as mybir
from concourse.masks import make_identity

P = 128
T = 1024
E = 8
C = 128
K, H, N = 1024, 512, 512
FLOPS = 2 * T * (K * H + H * N)

F32 = mybir.dt.float32
BF16 = mybir.dt.bfloat16
I32 = mybir.dt.int32
U32 = mybir.dt.uint32
U16 = mybir.dt.uint16
U8 = mybir.dt.uint8
FP8X4 = mybir.dt.float8_e4m3fn_x4
FP4X4 = mybir.dt.float4_e2m1fn_x4
ACT = mybir.ActivationFunctionType
MULT = mybir.AluOpType.mult
ADD = mybir.AluOpType.add


def runs(*sizes):
    edges = [sum(sizes[:i]) for i in range(len(sizes) + 1)]
    return [range(a, b) for a, b in zip(edges, edges[1:])]


XS_RUNS = runs(2, 6)
W1_RUNS = runs(1, 1, 2, 2, 2)
S1_RUNS = runs(3, 5)
XW_RUNS = runs(1, 1, 2, 4)
PUT_RUNS = runs(1, 1, 1, 1, 1, 3)
PART = 5 * T // 8
SUM_BANKS = "abfcbaed"
TURN_BANKS = "cacdbacb"
OUT_BANKS = "fghefghe"
Q_RUNS = runs(1, 2, 2, 1, 2)
SHARED = range(1, 5)
SPLITS = (3 * C, 3 * C)


def tile_moe_ser_gelu_kernel(
    tc, x_words, x_scales, w1_words, w1_scales, w2_words, w2_scales, gate1, gate2, offs, offs2, out
):
    nc = tc.nc

    def entries(lst, run):
        return lst[:, run.start * C // 16 : run.stop * C // 16]

    def slots(run):
        return slice(run.start * C, run.stop * C)

    def place(e, run):
        return slice((e - run.start) * C, (e - run.start + 1) * C)

    def one(e):
        return range(e, e + 1)

    with ExitStack() as ctx:
        lists = ctx.enter_context(tc.tile_pool(name="lists", bufs=1))
        keep = ctx.enter_context(tc.tile_pool(name="keep", bufs=1))
        psum = ctx.enter_context(tc.psum_pool(name="psum", bufs=1))

        list1 = lists.tile([P, T // 16], U16, name="list1")
        list2 = lists.tile([P, T // 16], U16, name="list2")
        nc.sync.dma_start(list1[:], offs)

        xs = keep.tile([P, T], U8, name="xs", align_bytes=64)
        nc.gpsimd.memset(xs[:].bitcast(I32), 0)
        ws_first = keep.tile([P, 2 * len(S1_RUNS[0]), H], U8, name="ws_first", align_bytes=64)
        nc.gpsimd.memset(ws_first[:].rearrange("p a n -> p (a n)").bitcast(I32), 0)
        g1_rows = keep.tile([P, P], F32, name="g1_rows", align_bytes=64)
        nc.gpsimd.memset(g1_rows[:], 0.0)
        nc.gpsimd.dma_start(g1_rows[0:E, :], gate1[0:1, :].rearrange("o (e u) -> (o e) u", e=E))
        ident = keep.tile([P, P], F32, name="ident")
        make_identity(nc, ident[:])
        ws = keep.tile([P, 2 * len(S1_RUNS[1]), H], U8, name="ws", align_bytes=64)
        nc.gpsimd.memset(ws[:].rearrange("p a n -> p (a n)").bitcast(I32), 0)

        def load_planes(tile, scales):
            rows = scales.rearrange("e s (q r) n -> r q (e s) n", r=4)
            for r in range(4):
                nc.sync.dma_start(tile[r:P:32, :, :].bitcast(I32), rows[r].bitcast(I32))

        def load_words(words, name):
            tile = keep.tile([P, words.shape[0] * words.shape[1], 2 * H], U8, name=name, align_bytes=64)
            nc.sync.dma_start(tile[:].bitcast(I32), words.rearrange("e s p n -> p (e s) n").bitcast(I32))
            return tile

        for q in range(4):
            nc.sync.dma_start(xs[32 * q : 32 * q + 8, :].bitcast(I32), x_scales[:, 4 * q : 4 * q + 4, :].bitcast(I32))
        nc.sync.dma_start(list2[:], offs2)
        xw = keep.tile([P, 2, T], I32, name="xw")
        nc.sync.dma_start(xw[:], x_words.rearrange("s p t d -> p s (t d)").bitcast(I32))
        w1w = {}

        def load_w1(run, name):
            tile = load_words(w1_words[run.start : run.stop], name)
            for e in run:
                w1w[e] = tile[:, 2 * (e - run.start) : 2 * (e - run.start) + 2, :]

        load_w1(W1_RUNS[0], "words_a")
        load_planes(ws_first, w1_scales[S1_RUNS[0].start : S1_RUNS[0].stop])
        load_w1(W1_RUNS[1], "words_b")

        xs_slot = {}
        for run in XS_RUNS:
            gathered = keep.tile([P, len(run) * C], U8, name=f"xs_pass0_{run.start}", align_bytes=64)
            shifted = keep.tile([P, len(run) * C], U8, name=f"xs_pass1_{run.start}", align_bytes=64)
            nc.vector.memset(shifted[:].bitcast(I32), 0)
            nc.vector.tensor_copy(gathered[:], xs[:].indirect(entries(list1, run)))
            nc.scalar.dma_start(shifted[0:100, :].bitcast(I32), gathered[4:104, :].bitcast(I32))
            for e in run:
                xs_slot[e, 0] = gathered[:, place(e, run)]
                xs_slot[e, 1] = shifted[:, place(e, run)]
        load_w1(W1_RUNS[2], "words_c")
        load_planes(ws, w1_scales[S1_RUNS[1].start : S1_RUNS[1].stop])
        w1s = {e: tile[:, 2 * (e - run.start) : 2 * (e - run.start) + 2, :] for run, tile in zip(S1_RUNS, [ws_first, ws]) for e in run}
        xw_slot = {}
        for run in XW_RUNS:
            for s in range(2):
                tile = keep.tile([P, len(run) * C], U32, name=f"xw_slot{run.start}_{s}", align_bytes=64)
                nc.vector.tensor_copy(tile[:], xw[:, s, :].bitcast(U32).indirect(entries(list1, run)))
                for e in run:
                    xw_slot[e, s] = tile[:, place(e, run)]

        g1_turned = psum.tile([P, P], F32, name="bank_d")
        nc.tensor.transpose(g1_turned[:], g1_rows[:], ident[:])
        g1 = keep.tile([P, E], F32, name="g1")
        nc.scalar.copy(g1[:], g1_turned[:, 0:E])

        load_w1(W1_RUNS[3], "g1_rows")
        c_slot = keep.tile([P, 2, T], F32, name="c_slot")
        c_both = {}

        def front(e):
            sums = psum.tile([P, H], F32, name="bank_" + SUM_BANKS[e])
            for s in range(2):
                nc.tensor.matmul_mx(
                    out=sums[:],
                    lhsT=xw_slot[e, s].bitcast(FP8X4),
                    lhsT_scale=xs_slot[e, s],
                    rhs=w1w[e][:, s, :].bitcast(FP4X4),
                    rhs_scale=w1s[e][:, s, :],
                    start=(s == 0),
                    stop=(s == 1),
                )
            if e == 0:
                load_w1(W1_RUNS[4], "words_a")
            h = keep.tile([P, 2, P, 2], F32, name=f"h{e}")
            by_pair = sums[:].rearrange("m (p u d) -> m u p d", u=2, d=2)
            c_both[e] = keep.tile([P, 2, 2 * P], BF16, name=f"c_both{e}")
            c_all = c_both[e][:].rearrange("m u i -> m (u i)")
            h_all = h[:].rearrange("m u p d -> m (u p d)")
            gate = g1[:, e : e + 1]
            if e == 0:
                for u in range(2):
                    nc.scalar.activation(h[:, u], by_pair[:, u], ACT.Gelu_apprx_tanh)
                nc.gpsimd.tensor_scalar(c_all[:, 0 : 2 * P], h_all[:, 0 : 2 * P], gate, 0.0, MULT, ADD)
                nc.scalar.activation(c_all[:, 2 * P :], h_all[:, 2 * P :], ACT.Copy, scale=gate)
            else:
                nc.scalar.activation(h[:], by_pair, ACT.Gelu_apprx_tanh)
                cut = 2 * P if e < 2 or e == E - 1 else P
                nc.scalar.activation(c_all[:, 0:cut], h_all[:, 0:cut], ACT.Copy, scale=gate)
                nc.gpsimd.tensor_scalar(c_all[:, cut:], h_all[:, cut:], gate, 0.0, MULT, ADD)

        def back(e):
            if e == 0:
                for u, bank in enumerate(["bank_c", "bank_e"]):
                    half = psum.tile([P, C], F32, name=bank)
                    nc.tensor.transpose(half[:], c_both[0][:, u, :].bitcast(F32), ident[:])
                    nc.scalar.copy(c_slot[:, u, 0:C], half[:])
                return
            turned = psum.tile([P, 2, C], F32, name="bank_" + TURN_BANKS[e])
            for u in range(2):
                nc.tensor.transpose(turned[:, u, :], c_both[e][:, u, :].bitcast(F32), ident[:])
            nc.scalar.copy(c_slot[:, :, slots(one(e))], turned[:])

        for e in range(E):
            front(e)
            if e < 2:
                back(e)
            elif e > 2:
                back(e - 1)
        back(E - 1)

        g2 = keep.tile([P, T], F32, name="xw_slot2_1", align_bytes=64)
        nc.sync.dma_start(g2[:], gate2)
        w2s = ws[:, 0:E, :]
        load_planes(w2s, w2_scales)
        w2w = load_words(w2_words, "words_b")

        c_tok = [keep.tile([P, T], F32, name=f"c_tok{u}") for u in range(2)]
        codes, scales = {}, {}
        wide = len(SHARED) * C
        dense1 = keep.tile([P, 2 * wide], U32, name="dense1", align_bytes=64)
        first = dense1[:, wide : wide + 2 * C]

        def gather(words, run, u):
            nc.vector.tensor_copy(words, c_tok[u][:].bitcast(U32).indirect(entries(list2, run)))

        for run in PUT_RUNS:
            for u in range(2):
                nc.vector.tensor_copy(c_tok[u][:].indirect(entries(list1, run)), c_slot[:, u, slots(run)])

        c_plane = keep.tile([P, 2, T], BF16, name="c_plane", align_bytes=64)
        halves = c_tok[0][:].bitcast(BF16).rearrange("p (t d) -> p d t", d=2)
        nc.scalar.copy(c_plane[:, :, 0:PART], halves[:, :, 0:PART])
        nc.gpsimd.tensor_scalar(c_plane[:, :, PART:], halves[:, :, PART:], 1.0, 0.0, MULT, ADD)

        y = keep.tile([P, 4, T], F32, name="y")

        def quantise(run, grouped):
            run_codes = keep.tile([P, len(run) * C], U32, name=f"codes{run.start}", align_bytes=64)
            run_scales = keep.tile([P, len(run) * C], U8, name=f"scales{run.start}", align_bytes=64)
            nc.vector.quantize_mx(out=run_codes[:].bitcast(FP8X4), scales=run_scales[:], in_=grouped)
            for e in run:
                codes[e] = run_codes[:, place(e, run)]
                scales[e] = run_scales[:, place(e, run)]

        def weave(run, name):
            woven = keep.tile([P, 2 * len(run) * C], F32, name=name, align_bytes=64)
            fours = slice((run.start - SHARED.start) * C // 4, (run.stop - SHARED.start) * C // 4)
            nc.vector.tensor_copy(
                woven[:].rearrange("p (c i u) -> p c u i", i=4, u=2),
                dense1[:].bitcast(F32).rearrange("p (u c i) -> p c u i", i=4, u=2)[:, fours],
            )
            quantise(run, woven[:].bitcast(BF16))

        def bring(run, name):
            words = keep.tile([P, 2 * len(run) * C], U32, name=name, align_bytes=64)
            for u in range(2):
                gather(words[:, u::2], run, u)
            quantise(run, words[:].bitcast(BF16))

        def products(f, blocks, bank):
            sums = psum.tile([P, len(blocks), C], F32, name="bank_" + bank)
            for b in blocks:
                nc.tensor.matmul_mx(
                    out=sums[:, b - blocks.start, :],
                    lhsT=w2w[:, f, 2 * P * b : 2 * P * (b + 1)].bitcast(FP4X4),
                    lhsT_scale=w2s[:, f, P * b : P * (b + 1)],
                    rhs=codes[f].bitcast(FP8X4),
                    rhs_scale=scales[f],
                    start=True,
                    stop=True,
                )
            for part in (range(0, 2), range(2, 4)) if f == E - 1 else (blocks,):
                gate = g2[:, slots(one(f))].unsqueeze(1).to_broadcast([P, len(part), C])
                part_sums = sums[:, part.start - blocks.start : part.stop - blocks.start, :]
                nc.vector.tensor_tensor(y[:, part.start : part.stop, slots(one(f))], part_sums, gate, MULT)

        for d in range(2):
            nc.scalar.activation(first.bitcast(BF16)[:, d::4], c_plane[:, d, :].indirect(entries(list2, Q_RUNS[0])), ACT.Copy)
        gather(first[:, 1::2], Q_RUNS[0], 1)
        quantise(Q_RUNS[0], first.bitcast(BF16))
        for d in range(2):
            nc.scalar.activation(dense1[:, 0:wide].bitcast(BF16)[:, d::2], c_plane[:, d, :].indirect(entries(list2, SHARED)), ACT.Copy)
        gather(dense1[:, wide:], SHARED, 1)
        products(0, range(0, 1), "a")
        products(0, range(1, 4), OUT_BANKS[0])
        weave(Q_RUNS[1], "codes0")
        weave(Q_RUNS[2], "scales0")
        bring(Q_RUNS[3], "codes0")
        products(1, range(4), OUT_BANKS[1])
        products(2, range(4), OUT_BANKS[2])
        bring(Q_RUNS[4], "codes1")
        for f in range(3, E):
            products(f, range(4), OUT_BANKS[f])

        out_tok = [keep.tile([P, T], F32, name=f"out_tok{b}") for b in range(4)]

        def listed(lo, hi):
            return list2[:, lo // 16 : hi // 16]

        def scatter_scalar(b, lo, hi):
            nc.scalar.activation(out_tok[b][:].indirect(listed(lo, hi)), y[:, b, lo:hi], ACT.Copy)

        def scatter_vector(b, lo, hi):
            nc.vector.tensor_copy(out_tok[b][:].indirect(listed(lo, hi)), y[:, b, lo:hi])

        def store(queue, b):
            queue.dma_start(out[P * b : P * (b + 1), :], out_tok[b][:])

        for b in range(4):
            scatter_scalar(b, 0, C)
        for b in (2, 3):
            scatter_scalar(b, C, 2 * C)
        for b in (0, 1):
            scatter_scalar(b, C, SPLITS[b])
        for b in (2, 3):
            scatter_scalar(b, 2 * C, 5 * C)
        for b in (0, 1):
            scatter_vector(b, SPLITS[b], T)
            store(nc.sync, b)
        for b in (2, 3):
            scatter_scalar(b, 5 * C, T)
            store(nc.scalar, b)
